import numpy as np
import ml_dtypes


def mxq(x, axis, fmt="e4m3"):
    dtype, down = {"e4m3": (ml_dtypes.float8_e4m3fn, 7), "e5m2": (ml_dtypes.float8_e5m2, 14)}[fmt]
    v = np.moveaxis(np.asarray(x, np.float32).astype(ml_dtypes.bfloat16).astype(np.float64), axis, -1)
    blocks = v.reshape(v.shape[:-1] + (-1, 32))
    amax = np.abs(blocks).max(-1, keepdims=True)
    byte = np.maximum(np.where(amax > 0, np.frexp(amax)[1] - 1 + 127, 0) - down, 1)
    scale = np.exp2(byte - 127.0)
    codes = (blocks / scale).astype(np.float32).astype(dtype).astype(np.float64)
    return np.moveaxis((codes * scale).reshape(v.shape), -1, axis)


WIDE = False


def mx_kscale(k):
    if not WIDE:
        return np.ones(k)
    levels = np.array([10, -10, 5, -5, 0])
    if k % 512:
        return np.exp2(np.random.permutation(np.resize(levels, k // 32))).repeat(32)
    a = np.empty((k // 512, 16))
    for p in range(k // 512):
        a[p, :8] = np.random.permutation(np.resize(levels, 8))
        for g in range(8):
            far = levels[np.abs(levels - a[p, g]) >= 10]
            a[p, g + 8] = far[np.random.randint(len(far))]
    return np.exp2(a.ravel()).repeat(32)


def f64(x):
    return np.asarray(x).astype(np.float64)


def striped(idx):
    return np.tile(idx.reshape(-1, 16).T, (8, 1)).astype(np.uint16)


def unstriped(offs):
    return offs[:16].T.reshape(-1).astype(np.int64)


def striped8(idx):
    return np.concatenate([x.reshape(-1, 16).T for x in idx]).astype(np.uint16)


def runs(offs, k):
    lists = np.stack([offs[16 * r : 16 * r + 16].T.reshape(-1) for r in range(8)]).astype(np.int64)
    return lists[np.arange(k) % 512 // 64]


def pack_weight(w):
    k, n = w.shape
    w = f64(np.asarray(w, np.float32).astype(ml_dtypes.bfloat16)).reshape(k // 32, 32, n)
    amax = np.abs(w).max(1)
    byte = np.clip(np.where(amax > 0, np.frexp(amax)[1] - 1 + 127 - 7, 1), 1, 254)
    scaled = (w * np.exp2(127.0 - byte)[:, None, :]).reshape(k, n).astype(np.float32)
    words = np.ascontiguousarray(scaled.reshape(k // 512, 128, 4, n).transpose(0, 1, 3, 2)).astype(ml_dtypes.float8_e4m3fn).view(np.uint8)
    return words, np.ascontiguousarray(byte.astype(np.uint8).reshape(k // 512, 16, n))


def unpack_weight(words, scales):
    g, p, n, _ = words.shape
    vals = np.ascontiguousarray(words).view(ml_dtypes.float8_e4m3fn).astype(np.float64) * np.repeat(np.exp2(scales.astype(np.float64) - 127.0), 8, axis=1)[..., None]
    return vals.transpose(0, 1, 3, 2).reshape(g * 512, n)

def planes(y):
    n, m = y.shape
    v = y.astype(np.float32).astype(ml_dtypes.bfloat16).astype(np.float64).reshape(n // 32, 32, m)
    top = np.abs(v).max(1)
    byte = np.clip(np.where(top > 0, np.frexp(top)[1] - 1 + 127 - 7, 1), 1, 254)
    codes = (v * np.exp2(127.0 - byte)[:, None, :]).reshape(n, m).astype(np.float32).astype(ml_dtypes.float8_e4m3fn).view(np.uint8)
    words = codes.reshape(n // 512, 128, 4, m).transpose(0, 1, 3, 2)
    return np.ascontiguousarray(words), np.ascontiguousarray(byte.astype(np.uint8).reshape(n // 512, 16, m))


K, T, S, N, H = 512, 2048, 512, 512, 512


def setup_inputs():
    n = np.random.standard_normal
    s = mx_kscale(K)[:, None]
    u = mx_kscale(H)
    packed_xT = pack_weight(n((K, T)) * s)
    packed_w1 = pack_weight(n((K, H)) / np.sqrt(K) / s)
    packed_w3 = pack_weight(n((H, N)) / np.sqrt(H) / u[:, None])
    return {
        "x_words": packed_xT[0],
        "x_scales": packed_xT[1],
        "w1_words": packed_w1[0],
        "w1_scales": packed_w1[1],
        "w2": (n((K, H)) / np.sqrt(K) / s * u).astype(np.float32),
        "other": (n((H, S)) * u[:, None]).astype(np.float32),
        "w3_words": packed_w3[0],
        "w3_scales": packed_w3[1],
        "offs": striped(np.random.permutation(T)[:S]),
        "perm": striped8(np.stack([np.random.permutation(S) for _ in range(8)])),
    }


def reference(x_words, x_scales, w1_words, w1_scales, w2, other, w3_words, w3_scales, offs, perm):
    xq = unpack_weight(x_words, x_scales)[:, unstriped(offs)]
    s = np.tanh(unpack_weight(w1_words, w1_scales).T @ xq)
    sh = mxq(f64(w2), 0, "e4m3").T @ xq
    z = (f64(other)[np.arange(H)[:, None], runs(perm, H)]) * np.exp(s) + sh
    out_0 = unpack_weight(w3_words, w3_scales).T @ mxq(z, 0, "e4m3")
    return (out_0,) + planes(out_0)

@@ -1,0 +1,224 @@
+from contextlib import ExitStack
+
+import concourse.mybir as mybir
+
+K, T, S, N, H = 512, 2048, 512, 512, 512
+FLOPS = 3 * 2 * 512 * 512 * 512
+
+F32 = mybir.dt.float32
+BF16 = mybir.dt.bfloat16
+I32 = mybir.dt.int32
+U32 = mybir.dt.uint32
+U16 = mybir.dt.uint16
+U8 = mybir.dt.uint8
+FP8X4 = mybir.dt.float8_e4m3fn_x4
+ACT = mybir.ActivationFunctionType
+ALU = mybir.AluOpType
+
+P = 128
+PACK = 4
+HALF = 256
+CH = 128
+
+
+def words_view(dram):
+    return dram[0].rearrange("p n t -> p (n t)").bitcast(I32)
+
+
+def load_scales(queue, tile, dram, first):
+    for q in range(4):
+        queue.dma_start(out=tile[32 * q + first : 32 * q + first + 4, :].bitcast(I32), in_=dram[0, 4 * q : 4 * q + 4, :].bitcast(I32))
+
+
+def deal(nc, out, in_, run):
+    nc.vector.tensor_copy(
+        out=out.rearrange("p (t c m) -> p c t m", t=PACK, m=run),
+        in_=in_.rearrange("p (c m t) -> p c t m", t=PACK, m=run),
+    )
+
+
+def tile_picked_nvp8_none_po_kernel(tc, x_words, x_scales, w1_words, w1_scales, w2, other, w3_words, w3_scales, offs, perm, out_0, out_1, out_2):
+    nc = tc.nc
+    with ExitStack() as ctx:
+        keep = ctx.enter_context(tc.tile_pool(name="keep", bufs=1))
+        psum = ctx.enter_context(tc.psum_pool(name="psum", bufs=1))
+
+        def tile(shape, dt, name, tag=None):
+            return keep.tile(shape, dt, name=name, tag=tag or name, align_bytes=64)
+
+        offs_t = tile([P, S // 16], U16, "offs_t")
+        perm_t = tile([P, S // 16], U16, "perm_t")
+        xw = tile([P, T], U32, "xw")
+        xs = tile([P, T], U8, "xs")
+        w1_raw = tile([P, H], U32, "w1_raw")
+        w3_raw = tile([P, N], U32, "w3_raw")
+        w1s_raw = tile([P, H], U8, "w1s_raw")
+        w3s_raw = tile([P, N], U8, "w3s_raw")
+        warm = tile([P, 8], F32, "warm")
+        warm_out = tile([P, 8], F32, "warm_out")
+        oth = [tile([P, S], F32, f"oth{t}") for t in range(PACK)]
+        w2_raw = tile([P, PACK, H], F32, "w2_raw")
+
+        nc.vector.memset(xs[:].bitcast(I32), 0)
+        nc.vector.memset(w1s_raw[:].bitcast(I32), 0)
+        nc.gpsimd.memset(w3s_raw[:].bitcast(I32), 0)
+        nc.vector.memset(warm[:], 0.0)
+
+        other_rows = other.rearrange("(p t) s -> p t s", t=PACK)
+        nc.sync.dma_start(offs_t[:], offs)
+        nc.sync.dma_start(perm_t[:], perm)
+        nc.sync.dma_start(out=xw[:].bitcast(I32), in_=words_view(x_words))
+        load_scales(nc.scalar, xs, x_scales, 0)
+        nc.sync.dma_start(out=w1_raw[:].bitcast(I32), in_=words_view(w1_words))
+        load_scales(nc.scalar, w1s_raw, w1_scales, 0)
+        load_scales(nc.gpsimd, w3s_raw, w3_scales, 0)
+        nc.scalar.activation(out=warm_out[:], in_=warm[:], func=ACT.Exp)
+        for t in (0, 1):
+            nc.sync.dma_start(out=oth[t][:], in_=other_rows[:, t, :])
+        nc.sync.dma_start(out=w2_raw[:], in_=w2.rearrange("(p j) c -> p j c", j=PACK))
+        for t in (2, 3):
+            nc.sync.dma_start(out=oth[t][:], in_=other_rows[:, t, :])
+        nc.sync.dma_start(out=w3_raw[:].bitcast(I32), in_=words_view(w3_words))
+
+        xq_s = tile([P, S], U8, "xq_s")
+        nc.vector.tensor_copy(out=xq_s[:], in_=xs[:].indirect(offs_t[:]))
+        w1s = tile([P, H], U8, "w1s")
+        deal(nc, w1s[:], w1s_raw[:], 16)
+        xq = [tile([P, HALF], U32, f"xq{h}") for h in range(2)]
+        nc.vector.tensor_copy(out=xq[0][:], in_=xw[:].indirect(offs_t[:, 0:16]))
+        w1c = tile([P, H], U32, "w1c")
+        deal(nc, w1c[:], w1_raw[:], 4)
+        nc.vector.tensor_copy(out=xq[1][:], in_=xw[:].indirect(offs_t[:, 16:32]))
+
+        prod = [tile([P, PACK, HALF], F32, f"prod{h}") for h in range(2)]
+        ex = {}
+
+        def scale_factor(h, pair):
+            bank = psum.tile([P, 2, HALF], F32, name=f"s{h}{pair}", tag=f"a{2 * pair + h}")
+            for u in range(2):
+                t = 2 * pair + u
+                nc.tensor.matmul_mx(
+                    out=bank[:, u, :],
+                    lhsT=w1c[:, t * P : (t + 1) * P].bitcast(FP8X4),
+                    lhsT_scale=w1s[:, t * P : (t + 1) * P],
+                    rhs=xq[h][:].bitcast(FP8X4),
+                    rhs_scale=xq_s[:, h * HALF : (h + 1) * HALF],
+                    start=True,
+                    stop=True,
+                )
+            th = tile([P, 2, HALF], F32, f"th{h}{pair}")
+            nc.scalar.activation(out=th[:], in_=bank[:], func=ACT.Tanh)
+            ex[h, pair] = tile([P, 2, HALF], F32, f"ex{h}{pair}")
+            nc.scalar.activation(out=ex[h, pair][:], in_=th[:], func=ACT.Exp)
+
+        def scaled_other(h, pair):
+            for u in range(2):
+                t = 2 * pair + u
+                nc.vector.tensor_tensor(prod[h][:, t, :], oth[t][:].indirect(perm_t[:, 16 * h : 16 * (h + 1)]), ex[h, pair][:, u, :], ALU.mult)
+
+        w2c = tile([P, H], U32, "w2c")
+        w2s = tile([P, H], U8, "w2s")
+        w2_v = w2_raw[:].rearrange("p j (m t) -> p m j t", t=PACK)
+
+        def round_w2(copy, pair, tag):
+            w2b = tile([P, 2 * P * PACK], BF16, f"w2b{pair}", tag)
+            copy(out=w2b[:].rearrange("p (t m j) -> p m j t", t=2, j=PACK), in_=w2_v[:, :, :, 2 * pair : 2 * pair + 2])
+            return w2b
+
+        def quantise_w2(w2b, pair):
+            cols = slice(2 * P * pair, 2 * P * (pair + 1))
+            nc.vector.quantize_mx(out=w2c[:, cols].bitcast(FP8X4), scales=w2s[:, cols], in_=w2b[:])
+
+        scale_factor(0, 0)
+        scaled_other(0, 0)
+        scale_factor(1, 0)
+        scaled_other(1, 0)
+        w2b0 = round_w2(nc.vector.tensor_copy, 0, "ex10")
+        scale_factor(0, 1)
+        w2b1 = round_w2(nc.scalar.copy, 1, "w2b1")
+        scaled_other(0, 1)
+        quantise_w2(w2b0, 0)
+        quantise_w2(w2b1, 1)
+        scale_factor(1, 1)
+
+        w3c = tile([P, N], U32, "w3c", "ex01")
+        deal(nc, w3c[:], w3_raw[:], 4)
+        w3s = tile([P, N], U8, "w3s", "th11")
+        deal(nc, w3s[:], w3s_raw[:], 16)
+
+        yc = tile([P, S], U32, "yc")
+        ys = tile([P, S], U8, "ys")
+        out_rows = out_0.rearrange("(p t) s -> p t s", t=PACK)
+        out_words = words_view(out_1)
+        zb = {}
+        yb = {}
+
+        def make_z(c):
+            h, off = divmod(c * CH, HALF)
+            cols = slice(c * CH, (c + 1) * CH)
+            sh = psum.tile([P, PACK, CH], F32, name=f"sh{c}", tag=f"b{c}")
+            for t in range(PACK):
+                nc.tensor.matmul_mx(
+                    out=sh[:, t, :],
+                    lhsT=w2c[:, t * P : (t + 1) * P].bitcast(FP8X4),
+                    lhsT_scale=w2s[:, t * P : (t + 1) * P],
+                    rhs=xq[h][:, off : off + CH].bitcast(FP8X4),
+                    rhs_scale=xq_s[:, cols],
+                    start=True,
+                    stop=True,
+                )
+            zb[c] = tile([P, CH * PACK], BF16, f"zb{c}")
+            nc.vector.tensor_tensor(
+                zb[c][:].rearrange("p (g i t) -> p g t i", t=PACK, i=4),
+                sh[:].rearrange("p t (g i) -> p g t i", i=4),
+                prod[h][:, :, off : off + CH].rearrange("p t (g i) -> p g t i", i=4),
+                ALU.add,
+            )
+
+        def last_layer(c, by_vector):
+            cols = slice(c * CH, (c + 1) * CH)
+            zc = tile([P, CH], U32, f"zc{c}")
+            zs = tile([P, CH], U8, f"zs{c}")
+            nc.vector.quantize_mx(out=zc[:].bitcast(FP8X4), scales=zs[:], in_=zb[c][:])
+            acc = psum.tile([P, PACK, CH], F32, name=f"acc{c}", tag=f"a{c}")
+            for t in range(PACK):
+                nc.tensor.matmul_mx(
+                    out=acc[:, t, :],
+                    lhsT=w3c[:, t * P : (t + 1) * P].bitcast(FP8X4),
+                    lhsT_scale=w3s[:, t * P : (t + 1) * P],
+                    rhs=zc[:].bitcast(FP8X4),
+                    rhs_scale=zs[:],
+                    start=True,
+                    stop=True,
+                )
+            y = tile([P, PACK, CH], F32, f"y{c}")
+            nc.scalar.copy(out=y[:], in_=acc[:])
+            nc.sync.dma_start(out=out_rows[:, :, cols], in_=y[:])
+            yb[c] = tile([P, CH * PACK], BF16, f"yb{c}")
+            grouped = yb[c][:].rearrange("p (g i t) -> p g t i", t=PACK, i=4)
+            if by_vector:
+                nc.vector.tensor_copy(out=grouped, in_=y[:].rearrange("p t (g i) -> p g t i", i=4))
+            else:
+                nc.scalar.copy(out=grouped, in_=acc[:].rearrange("p t (g i) -> p g t i", i=4))
+
+        def planes(c):
+            cols = slice(c * CH, (c + 1) * CH)
+            nc.vector.quantize_mx(out=yc[:, cols].bitcast(FP8X4), scales=ys[:, cols], in_=yb[c][:])
+            nc.sync.dma_start(out=out_words[:, cols], in_=yc[:, cols].bitcast(I32))
+
+        make_z(0)
+        make_z(1)
+        last_layer(0, False)
+        last_layer(1, False)
+        scaled_other(1, 1)
+        make_z(2)
+        planes(0)
+        make_z(3)
+        last_layer(2, True)
+        planes(1)
+        last_layer(3, True)
+        planes(2)
+        planes(3)
+        for q in range(4):
+            queue = nc.sync if q % 2 == 0 else nc.scalar
+            queue.dma_start(out=out_2[0, 4 * q : 4 * q + 4, :].bitcast(I32), in_=ys[32 * q : 32 * q + 4, :].bitcast(I32))

@@ -25,9 +25,9 @@ def words_view(dram):
     return dram[0].rearrange("p n t -> p (n t)").bitcast(I32)
 
 
-def load_scales(queue, tile, dram, first):
-    for q in range(4):
-        queue.dma_start(out=tile[32 * q + first : 32 * q + first + 4, :].bitcast(I32), in_=dram[0, 4 * q : 4 * q + 4, :].bitcast(I32))
+def load_scales(queue, tile, dram, quadrants):
+    for q in quadrants:
+        queue.dma_start(out=tile[32 * q : 32 * q + 4, :].bitcast(I32), in_=dram[0, 4 * q : 4 * q + 4, :].bitcast(I32))
 
 
 def deal(nc, out, in_, run):
@@ -51,70 +51,83 @@ def tile_picked_nvp8_none_po_kernel(tc, x_words, x_scales, w1_words, w1_scales, 
         xw = tile([P, T], U32, "xw")
         xs = tile([P, T], U8, "xs")
         w1_raw = tile([P, H], U32, "w1_raw")
-        w3_raw = tile([P, N], U32, "w3_raw")
         w1s_raw = tile([P, H], U8, "w1s_raw")
         w3s_raw = tile([P, N], U8, "w3s_raw")
         warm = tile([P, 8], F32, "warm")
         warm_out = tile([P, 8], F32, "warm_out")
-        oth = [tile([P, S], F32, f"oth{t}") for t in range(PACK)]
-        w2_raw = tile([P, PACK, H], F32, "w2_raw")
 
         nc.vector.memset(xs[:].bitcast(I32), 0)
-        nc.vector.memset(w1s_raw[:].bitcast(I32), 0)
+        nc.gpsimd.memset(w1s_raw[:].bitcast(I32), 0)
         nc.gpsimd.memset(w3s_raw[:].bitcast(I32), 0)
         nc.vector.memset(warm[:], 0.0)
 
         other_rows = other.rearrange("(p t) s -> p t s", t=PACK)
         nc.sync.dma_start(offs_t[:], offs)
         nc.sync.dma_start(perm_t[:], perm)
-        nc.sync.dma_start(out=xw[:].bitcast(I32), in_=words_view(x_words))
-        load_scales(nc.scalar, xs, x_scales, 0)
         nc.sync.dma_start(out=w1_raw[:].bitcast(I32), in_=words_view(w1_words))
-        load_scales(nc.scalar, w1s_raw, w1_scales, 0)
-        load_scales(nc.gpsimd, w3s_raw, w3_scales, 0)
+        load_scales(nc.scalar, xs, x_scales, (0, 1))
+        load_scales(nc.sync, xs, x_scales, (2, 3))
+        nc.sync.dma_start(out=xw[:].bitcast(I32), in_=words_view(x_words))
+        load_scales(nc.gpsimd, w1s_raw, w1_scales, (3,))
+        load_scales(nc.sync, w1s_raw, w1_scales, range(3))
+        load_scales(nc.gpsimd, w3s_raw, w3_scales, range(4))
         nc.scalar.activation(out=warm_out[:], in_=warm[:], func=ACT.Exp)
-        for t in (0, 1):
-            nc.sync.dma_start(out=oth[t][:], in_=other_rows[:, t, :])
-        nc.sync.dma_start(out=w2_raw[:], in_=w2.rearrange("(p j) c -> p j c", j=PACK))
-        for t in (2, 3):
-            nc.sync.dma_start(out=oth[t][:], in_=other_rows[:, t, :])
-        nc.sync.dma_start(out=w3_raw[:].bitcast(I32), in_=words_view(w3_words))
 
-        xq_s = tile([P, S], U8, "xq_s")
-        nc.vector.tensor_copy(out=xq_s[:], in_=xs[:].indirect(offs_t[:]))
-        w1s = tile([P, H], U8, "w1s")
-        deal(nc, w1s[:], w1s_raw[:], 16)
-        xq = [tile([P, HALF], U32, f"xq{h}") for h in range(2)]
-        nc.vector.tensor_copy(out=xq[0][:], in_=xw[:].indirect(offs_t[:, 0:16]))
+        oth = {}
+
+        def load_other(t, tag):
+            oth[t] = tile([P, S], F32, f"oth{t}", tag)
+            nc.sync.dma_start(out=oth[t][:], in_=other_rows[:, t, :])
+
+        w3_raw = tile([P, N], U32, "w3_raw", "warm_out")
+        nc.sync.dma_start(out=w3_raw[:].bitcast(I32), in_=words_view(w3_words))
+        load_other(0, "warm")
+
         w1c = tile([P, H], U32, "w1c")
         deal(nc, w1c[:], w1_raw[:], 4)
+        load_other(1, "w1_raw")
+        xq_s = tile([P, S], U8, "xq_s")
+        nc.vector.tensor_copy(out=xq_s[:], in_=xs[:].indirect(offs_t[:]))
+        w2_raw = tile([P, PACK, H], F32, "w2_raw", "xs")
+        nc.sync.dma_start(out=w2_raw[:], in_=w2.rearrange("(p j) c -> p j c", j=PACK))
+        xq = [tile([P, HALF], U32, "xq0")]
+        nc.vector.tensor_copy(out=xq[0][:], in_=xw[:].indirect(offs_t[:, 0:16]))
+        w1s = tile([P, H], U8, "w1s")
+        deal(nc, w1s[:], w1s_raw[:], 16)
+        xq.append(tile([P, HALF], U32, "xq1", "w1s_raw"))
         nc.vector.tensor_copy(out=xq[1][:], in_=xw[:].indirect(offs_t[:, 16:32]))
+        w3c = tile([P, N], U32, "w3c")
+        deal(nc, w3c[:], w3_raw[:], 4)
+        load_other(2, "xw")
+        load_other(3, "warm_out")
 
         prod = [tile([P, PACK, HALF], F32, f"prod{h}") for h in range(2)]
+        units = [(h, 2 * pair + u) for pair in range(2) for h in range(2) for u in range(2)]
+        th = {}
         ex = {}
 
-        def scale_factor(h, pair):
-            bank = psum.tile([P, 2, HALF], F32, name=f"s{h}{pair}", tag=f"a{2 * pair + h}")
-            for u in range(2):
-                t = 2 * pair + u
-                nc.tensor.matmul_mx(
-                    out=bank[:, u, :],
-                    lhsT=w1c[:, t * P : (t + 1) * P].bitcast(FP8X4),
-                    lhsT_scale=w1s[:, t * P : (t + 1) * P],
-                    rhs=xq[h][:].bitcast(FP8X4),
-                    rhs_scale=xq_s[:, h * HALF : (h + 1) * HALF],
-                    start=True,
-                    stop=True,
-                )
-            th = tile([P, 2, HALF], F32, f"th{h}{pair}")
-            nc.scalar.activation(out=th[:], in_=bank[:], func=ACT.Tanh)
-            ex[h, pair] = tile([P, 2, HALF], F32, f"ex{h}{pair}")
-            nc.scalar.activation(out=ex[h, pair][:], in_=th[:], func=ACT.Exp)
+        def tanh_unit(i):
+            h, t = units[i]
+            bank = psum.tile([P, HALF], F32, name=f"s{i}", tag=f"bank{i}")
+            nc.tensor.matmul_mx(
+                out=bank[:],
+                lhsT=w1c[:, t * P : (t + 1) * P].bitcast(FP8X4),
+                lhsT_scale=w1s[:, t * P : (t + 1) * P],
+                rhs=xq[h][:].bitcast(FP8X4),
+                rhs_scale=xq_s[:, h * HALF : (h + 1) * HALF],
+                start=True,
+                stop=True,
+            )
+            th[i] = tile([P, HALF], F32, f"th{i}")
+            nc.scalar.activation(out=th[i][:], in_=bank[:], func=ACT.Tanh)
 
-        def scaled_other(h, pair):
-            for u in range(2):
-                t = 2 * pair + u
-                nc.vector.tensor_tensor(prod[h][:, t, :], oth[t][:].indirect(perm_t[:, 16 * h : 16 * (h + 1)]), ex[h, pair][:, u, :], ALU.mult)
+        def exp_unit(i):
+            ex[i] = tile([P, HALF], F32, f"ex{i}")
+            nc.scalar.activation(out=ex[i][:], in_=th[i][:], func=ACT.Exp)
+
+        def scaled_other(i):
+            h, t = units[i]
+            nc.vector.tensor_tensor(prod[h][:, t, :], oth[t][:].indirect(perm_t[:, 16 * h : 16 * (h + 1)]), ex[i][:], ALU.mult)
 
         w2c = tile([P, H], U32, "w2c")
         w2s = tile([P, H], U8, "w2s")
@@ -129,96 +142,114 @@ def tile_picked_nvp8_none_po_kernel(tc, x_words, x_scales, w1_words, w1_scales, 
             cols = slice(2 * P * pair, 2 * P * (pair + 1))
             nc.vector.quantize_mx(out=w2c[:, cols].bitcast(FP8X4), scales=w2s[:, cols], in_=w2b[:])
 
-        scale_factor(0, 0)
-        scaled_other(0, 0)
-        scale_factor(1, 0)
-        scaled_other(1, 0)
-        w2b0 = round_w2(nc.vector.tensor_copy, 0, "ex10")
-        scale_factor(0, 1)
+        tanh_unit(0)
+        for i in range(5):
+            tanh_unit(i + 1)
+            exp_unit(i)
+            if i < 4:
+                scaled_other(i)
+        exp_unit(5)
+        w2b0 = round_w2(nc.vector.tensor_copy, 0, "ex3")
         w2b1 = round_w2(nc.scalar.copy, 1, "w2b1")
-        scaled_other(0, 1)
+        scaled_other(4)
+        scaled_other(5)
         quantise_w2(w2b0, 0)
         quantise_w2(w2b1, 1)
-        scale_factor(1, 1)
-
-        w3c = tile([P, N], U32, "w3c", "ex01")
-        deal(nc, w3c[:], w3_raw[:], 4)
-        w3s = tile([P, N], U8, "w3s", "th11")
+        tanh_unit(6)
+        tanh_unit(7)
+        exp_unit(6)
+        exp_unit(7)
+        scaled_other(6)
+        scaled_other(7)
+        w3s = tile([P, N], U8, "w3s", "th7")
         deal(nc, w3s[:], w3s_raw[:], 16)
 
         yc = tile([P, S], U32, "yc")
         ys = tile([P, S], U8, "ys")
         out_rows = out_0.rearrange("(p t) s -> p t s", t=PACK)
         out_words = words_view(out_1)
-        zb = {}
-        yb = {}
+        zb = [tile([P, HALF * PACK], BF16, f"zb{h}") for h in range(2)]
+        zc = [tile([P, HALF], U32, f"zc{h}") for h in range(2)]
+        zs = [tile([P, HALF], U8, f"zs{h}") for h in range(2)]
+        yb = [tile([P, HALF * PACK], BF16, f"yb{h}") for h in range(2)]
+        y = [tile([P, PACK, CH], F32, f"y{c}") for c in range(4)]
 
         def make_z(c):
             h, off = divmod(c * CH, HALF)
-            cols = slice(c * CH, (c + 1) * CH)
-            sh = psum.tile([P, PACK, CH], F32, name=f"sh{c}", tag=f"b{c}")
+            sh = psum.tile([P, PACK, CH], F32, name=f"sh{c}", tag=f"bank{c}")
             for t in range(PACK):
                 nc.tensor.matmul_mx(
                     out=sh[:, t, :],
                     lhsT=w2c[:, t * P : (t + 1) * P].bitcast(FP8X4),
                     lhsT_scale=w2s[:, t * P : (t + 1) * P],
                     rhs=xq[h][:, off : off + CH].bitcast(FP8X4),
-                    rhs_scale=xq_s[:, cols],
+                    rhs_scale=xq_s[:, c * CH : (c + 1) * CH],
                     start=True,
                     stop=True,
                 )
-            zb[c] = tile([P, CH * PACK], BF16, f"zb{c}")
             nc.vector.tensor_tensor(
-                zb[c][:].rearrange("p (g i t) -> p g t i", t=PACK, i=4),
-                sh[:].rearrange("p t (g i) -> p g t i", i=4),
-                prod[h][:, :, off : off + CH].rearrange("p t (g i) -> p g t i", i=4),
+                zb[h][:, off * PACK : (off + CH) * PACK].rearrange("p (g i t) -> p g t i", t=PACK, i=2),
+                sh[:].rearrange("p t (g i) -> p g t i", i=2),
+                prod[h][:, :, off : off + CH].rearrange("p t (g i) -> p g t i", i=2),
                 ALU.add,
             )
 
-        def last_layer(c, by_vector):
-            cols = slice(c * CH, (c + 1) * CH)
-            zc = tile([P, CH], U32, f"zc{c}")
-            zs = tile([P, CH], U8, f"zs{c}")
-            nc.vector.quantize_mx(out=zc[:].bitcast(FP8X4), scales=zs[:], in_=zb[c][:])
-            acc = psum.tile([P, PACK, CH], F32, name=f"acc{c}", tag=f"a{c}")
+        def quantise_z(h, off, width):
+            nc.vector.quantize_mx(
+                out=zc[h][:, off : off + width].bitcast(FP8X4), scales=zs[h][:, off : off + width], in_=zb[h][:, off * PACK : (off + width) * PACK]
+            )
+
+        def last_layer(c):
+            h, off = divmod(c * CH, HALF)
+            acc = psum.tile([P, PACK, CH], F32, name=f"acc{c}", tag=f"bank{4 + c}")
             for t in range(PACK):
                 nc.tensor.matmul_mx(
                     out=acc[:, t, :],
                     lhsT=w3c[:, t * P : (t + 1) * P].bitcast(FP8X4),
                     lhsT_scale=w3s[:, t * P : (t + 1) * P],
-                    rhs=zc[:].bitcast(FP8X4),
-                    rhs_scale=zs[:],
+                    rhs=zc[h][:, off : off + CH].bitcast(FP8X4),
+                    rhs_scale=zs[h][:, off : off + CH],
                     start=True,
                     stop=True,
                 )
-            y = tile([P, PACK, CH], F32, f"y{c}")
-            nc.scalar.copy(out=y[:], in_=acc[:])
-            nc.sync.dma_start(out=out_rows[:, :, cols], in_=y[:])
-            yb[c] = tile([P, CH * PACK], BF16, f"yb{c}")
-            grouped = yb[c][:].rearrange("p (g i t) -> p g t i", t=PACK, i=4)
-            if by_vector:
-                nc.vector.tensor_copy(out=grouped, in_=y[:].rearrange("p t (g i) -> p g t i", i=4))
-            else:
-                nc.scalar.copy(out=grouped, in_=acc[:].rearrange("p t (g i) -> p g t i", i=4))
+            nc.scalar.copy(out=y[c][:], in_=acc[:])
+            nc.sync.dma_start(out=out_rows[:, :, c * CH : (c + 1) * CH], in_=y[c][:])
 
-        def planes(c):
-            cols = slice(c * CH, (c + 1) * CH)
-            nc.vector.quantize_mx(out=yc[:, cols].bitcast(FP8X4), scales=ys[:, cols], in_=yb[c][:])
+        def round_y(c):
+            h, off = divmod(c * CH, HALF)
+            nc.vector.tensor_copy(
+                out=yb[h][:, off * PACK : (off + CH) * PACK].rearrange("p (g i t) -> p g t i", t=PACK, i=4),
+                in_=y[c][:].rearrange("p t (g i) -> p g t i", i=4),
+            )
+
+        def quantise_y(h, off, width):
+            cols = slice(h * HALF + off, h * HALF + off + width)
+            nc.vector.quantize_mx(out=yc[:, cols].bitcast(FP8X4), scales=ys[:, cols], in_=yb[h][:, off * PACK : (off + width) * PACK])
+
+        def store_words(h):
+            cols = slice(h * HALF, (h + 1) * HALF)
             nc.sync.dma_start(out=out_words[:, cols], in_=yc[:, cols].bitcast(I32))
 
         make_z(0)
         make_z(1)
-        last_layer(0, False)
-        last_layer(1, False)
-        scaled_other(1, 1)
         make_z(2)
-        planes(0)
+        quantise_z(0, 0, HALF)
+        last_layer(0)
+        last_layer(1)
         make_z(3)
-        last_layer(2, True)
-        planes(1)
-        last_layer(3, True)
-        planes(2)
-        planes(3)
+        quantise_z(1, 0, CH)
+        last_layer(2)
+        quantise_z(1, CH, CH)
+        last_layer(3)
+        round_y(0)
+        round_y(1)
+        round_y(2)
+        quantise_y(0, 0, HALF)
+        store_words(0)
+        round_y(3)
+        quantise_y(1, 0, CH)
+        quantise_y(1, CH, CH)
+        store_words(1)
         for q in range(4):
-            queue = nc.sync if q % 2 == 0 else nc.scalar
+            queue = nc.scalar if q < 2 else nc.sync
             queue.dma_start(out=out_2[0, 4 * q : 4 * q + 4, :].bitcast(I32), in_=ys[32 * q : 32 * q + 4, :].bitcast(I32))

@@ -226,15 +226,12 @@ def tile_picked_nvp8_none_po_kernel(tc, x_words, x_scales, w1_words, w1_scales, 
             cols = slice(h * HALF + off, h * HALF + off + width)
             nc.vector.quantize_mx(out=yc[:, cols].bitcast(FP8X4), scales=ys[:, cols], in_=yb[h][:, off * PACK : (off + width) * PACK])
 
-        def store_words(h):
-            cols = slice(h * HALF, (h + 1) * HALF)
-            nc.sync.dma_start(out=out_words[:, cols], in_=yc[:, cols].bitcast(I32))
-
         make_z(0)
         make_z(1)
-        make_z(2)
-        quantise_z(0, 0, HALF)
+        quantise_z(0, 0, CH)
         last_layer(0)
+        make_z(2)
+        quantise_z(0, CH, CH)
         last_layer(1)
         make_z(3)
         quantise_z(1, 0, CH)
@@ -245,11 +242,10 @@ def tile_picked_nvp8_none_po_kernel(tc, x_words, x_scales, w1_words, w1_scales, 
         round_y(1)
         round_y(2)
         quantise_y(0, 0, HALF)
-        store_words(0)
         round_y(3)
         quantise_y(1, 0, CH)
         quantise_y(1, CH, CH)
-        store_words(1)
+        nc.sync.dma_start(out=out_words, in_=yc[:].bitcast(I32))
         for q in range(4):
             queue = nc.scalar if q < 2 else nc.sync
             queue.dma_start(out=out_2[0, 4 * q : 4 * q + 4, :].bitcast(I32), in_=ys[32 * q : 32 * q + 4, :].bitcast(I32))

@@ -133,14 +133,9 @@ def tile_picked_nvp8_none_po_kernel(tc, x_words, x_scales, w1_words, w1_scales, 
         w2s = tile([P, H], U8, "w2s")
         w2_v = w2_raw[:].rearrange("p j (m t) -> p m j t", t=PACK)
 
-        def round_w2(copy, pair, tag):
-            w2b = tile([P, 2 * P * PACK], BF16, f"w2b{pair}", tag)
-            copy(out=w2b[:].rearrange("p (t m j) -> p m j t", t=2, j=PACK), in_=w2_v[:, :, :, 2 * pair : 2 * pair + 2])
-            return w2b
-
-        def quantise_w2(w2b, pair):
-            cols = slice(2 * P * pair, 2 * P * (pair + 1))
-            nc.vector.quantize_mx(out=w2c[:, cols].bitcast(FP8X4), scales=w2s[:, cols], in_=w2b[:])
+        def round_w2(copy, pair):
+            planes = slice(2 * pair, 2 * pair + 2)
+            copy(out=w2b[:].rearrange("p (t m j) -> p m j t", t=PACK, j=PACK)[:, :, :, planes], in_=w2_v[:, :, :, planes])
 
         tanh_unit(0)
         for i in range(5):
@@ -149,12 +144,12 @@ def tile_picked_nvp8_none_po_kernel(tc, x_words, x_scales, w1_words, w1_scales, 
             if i < 4:
                 scaled_other(i)
         exp_unit(5)
-        w2b0 = round_w2(nc.vector.tensor_copy, 0, "ex3")
-        w2b1 = round_w2(nc.scalar.copy, 1, "w2b1")
+        w2b = tile([P, H * PACK], BF16, "w2b", "ex3")
+        round_w2(nc.vector.tensor_copy, 0)
+        round_w2(nc.scalar.copy, 1)
         scaled_other(4)
         scaled_other(5)
-        quantise_w2(w2b0, 0)
-        quantise_w2(w2b1, 1)
+        nc.vector.quantize_mx(out=w2c[:].bitcast(FP8X4), scales=w2s[:], in_=w2b[:])
         tanh_unit(6)
         tanh_unit(7)
         exp_unit(6)

@@ -17,8 +17,13 @@ ALU = mybir.AluOpType
 
 P = 128
 PACK = 4
+QUADRANTS = 4
 HALF = 256
-CH = 128
+CHUNK = 128
+CHUNKS = S // CHUNK
+LIST_HALF = HALF // 16
+LINE = 16
+PLANE_BYTES = 4 * S
 
 
 def words_view(dram):
@@ -41,25 +46,26 @@ def tile_picked_nvp8_none_po_kernel(tc, x_words, x_scales, w1_words, w1_scales, 
     nc = tc.nc
     with ExitStack() as ctx:
         keep = ctx.enter_context(tc.tile_pool(name="keep", bufs=1))
+        stage = ctx.enter_context(tc.tile_pool(name="stage", bufs=1))
         psum = ctx.enter_context(tc.psum_pool(name="psum", bufs=1))
 
         def tile(shape, dt, name, tag=None):
             return keep.tile(shape, dt, name=name, tag=tag or name, align_bytes=64)
 
+        def staged(shape, dt, name, place):
+            return stage.tile(shape, dt, name=name, tag=name, align_bytes=64, offset=PLANE_BYTES * place)
+
         offs_t = tile([P, S // 16], U16, "offs_t")
         perm_t = tile([P, S // 16], U16, "perm_t")
         xw = tile([P, T], U32, "xw")
         xs = tile([P, T], U8, "xs")
-        w1_raw = tile([P, H], U32, "w1_raw")
+        w1_raw = staged([P, 4 * H], U32, "w1_raw", 0)[:, :H]
         w1s_raw = tile([P, H], U8, "w1s_raw")
         w3s_raw = tile([P, N], U8, "w3s_raw")
-        warm = tile([P, 8], F32, "warm")
-        warm_out = tile([P, 8], F32, "warm_out")
 
         nc.vector.memset(xs[:].bitcast(I32), 0)
         nc.gpsimd.memset(w1s_raw[:].bitcast(I32), 0)
         nc.gpsimd.memset(w3s_raw[:].bitcast(I32), 0)
-        nc.vector.memset(warm[:], 0.0)
 
         other_rows = other.rearrange("(p t) s -> p t s", t=PACK)
         nc.sync.dma_start(offs_t[:], offs)
@@ -70,36 +76,35 @@ def tile_picked_nvp8_none_po_kernel(tc, x_words, x_scales, w1_words, w1_scales, 
         nc.sync.dma_start(out=xw[:].bitcast(I32), in_=words_view(x_words))
         load_scales(nc.gpsimd, w1s_raw, w1_scales, (3,))
         load_scales(nc.sync, w1s_raw, w1_scales, range(3))
-        load_scales(nc.gpsimd, w3s_raw, w3_scales, range(4))
-        nc.scalar.activation(out=warm_out[:], in_=warm[:], func=ACT.Exp)
+        load_scales(nc.gpsimd, w3s_raw, w3_scales, range(QUADRANTS))
 
         oth = {}
 
-        def load_other(t, tag):
-            oth[t] = tile([P, S], F32, f"oth{t}", tag)
-            nc.sync.dma_start(out=oth[t][:], in_=other_rows[:, t, :])
-
-        w3_raw = tile([P, N], U32, "w3_raw", "warm_out")
-        nc.sync.dma_start(out=w3_raw[:].bitcast(I32), in_=words_view(w3_words))
-        load_other(0, "warm")
+        def load_other(t, plane):
+            oth[t] = plane
+            nc.sync.dma_start(out=plane[:], in_=other_rows[:, t, :])
 
         w1c = tile([P, H], U32, "w1c")
-        deal(nc, w1c[:], w1_raw[:], 4)
-        load_other(1, "w1_raw")
+        deal(nc, w1c[:], w1_raw[:], LINE // 4)
+        w3_raw = staged([P, N], U32, "w3_raw", 1)
+        nc.sync.dma_start(out=w3_raw[:].bitcast(I32), in_=words_view(w3_words))
+        load_other(0, staged([P, S], F32, "oth0", 2))
+        load_other(1, staged([P, S], F32, "oth1", 3))
+
         xq_s = tile([P, S], U8, "xq_s")
         nc.vector.tensor_copy(out=xq_s[:], in_=xs[:].indirect(offs_t[:]))
         w2_raw = tile([P, PACK, H], F32, "w2_raw", "xs")
         nc.sync.dma_start(out=w2_raw[:], in_=w2.rearrange("(p j) c -> p j c", j=PACK))
         xq = [tile([P, HALF], U32, "xq0")]
-        nc.vector.tensor_copy(out=xq[0][:], in_=xw[:].indirect(offs_t[:, 0:16]))
+        nc.vector.tensor_copy(out=xq[0][:], in_=xw[:].indirect(offs_t[:, :LIST_HALF]))
         w1s = tile([P, H], U8, "w1s")
-        deal(nc, w1s[:], w1s_raw[:], 16)
+        deal(nc, w1s[:], w1s_raw[:], LINE)
         xq.append(tile([P, HALF], U32, "xq1", "w1s_raw"))
-        nc.vector.tensor_copy(out=xq[1][:], in_=xw[:].indirect(offs_t[:, 16:32]))
+        nc.vector.tensor_copy(out=xq[1][:], in_=xw[:].indirect(offs_t[:, LIST_HALF:]))
         w3c = tile([P, N], U32, "w3c")
-        deal(nc, w3c[:], w3_raw[:], 4)
-        load_other(2, "xw")
-        load_other(3, "warm_out")
+        deal(nc, w3c[:], w3_raw[:], LINE // 4)
+        load_other(2, tile([P, S], F32, "oth2", "xw"))
+        load_other(3, staged([P, S], F32, "oth3", 1))
 
         prod = [tile([P, PACK, HALF], F32, f"prod{h}") for h in range(2)]
         units = [(h, 2 * pair + u) for pair in range(2) for h in range(2) for u in range(2)]
@@ -127,37 +132,39 @@ def tile_picked_nvp8_none_po_kernel(tc, x_words, x_scales, w1_words, w1_scales, 
 
         def scaled_other(i):
             h, t = units[i]
-            nc.vector.tensor_tensor(prod[h][:, t, :], oth[t][:].indirect(perm_t[:, 16 * h : 16 * (h + 1)]), ex[i][:], ALU.mult)
+            lists = perm_t[:, LIST_HALF * h : LIST_HALF * (h + 1)]
+            nc.vector.tensor_tensor(prod[h][:, t, :], oth[t][:].indirect(lists), ex[i][:], ALU.mult)
 
         w2c = tile([P, H], U32, "w2c")
         w2s = tile([P, H], U8, "w2s")
-        w2_v = w2_raw[:].rearrange("p j (m t) -> p m j t", t=PACK)
 
         def round_w2(copy, pair):
             planes = slice(2 * pair, 2 * pair + 2)
-            copy(out=w2b[:].rearrange("p (t m j) -> p m j t", t=PACK, j=PACK)[:, :, :, planes], in_=w2_v[:, :, :, planes])
+            copy(
+                out=w2b[:].rearrange("p (t m j) -> p m j t", t=PACK, j=PACK)[:, :, :, planes],
+                in_=w2_raw[:].rearrange("p j (m t) -> p m j t", t=PACK)[:, :, :, planes],
+            )
 
+        early_units = len(units) // 2
+        before_rounding = early_units + 2
         tanh_unit(0)
-        for i in range(5):
+        for i in range(before_rounding - 1):
             tanh_unit(i + 1)
             exp_unit(i)
-            if i < 4:
+            if i < early_units:
                 scaled_other(i)
-        exp_unit(5)
-        w2b = tile([P, H * PACK], BF16, "w2b", "ex3")
+        exp_unit(before_rounding - 1)
+        w2b = tile([P, H * PACK], BF16, "w2b", f"ex{early_units - 1}")
         round_w2(nc.vector.tensor_copy, 0)
         round_w2(nc.scalar.copy, 1)
-        scaled_other(4)
-        scaled_other(5)
+        for i in range(early_units, before_rounding):
+            scaled_other(i)
         nc.vector.quantize_mx(out=w2c[:].bitcast(FP8X4), scales=w2s[:], in_=w2b[:])
-        tanh_unit(6)
-        tanh_unit(7)
-        exp_unit(6)
-        exp_unit(7)
-        scaled_other(6)
-        scaled_other(7)
-        w3s = tile([P, N], U8, "w3s", "th7")
-        deal(nc, w3s[:], w3s_raw[:], 16)
+        for step in (tanh_unit, exp_unit, scaled_other):
+            for i in range(before_rounding, len(units)):
+                step(i)
+        w3s = tile([P, N], U8, "w3s", f"th{len(units) - 1}")
+        deal(nc, w3s[:], w3s_raw[:], LINE)
 
         yc = tile([P, S], U32, "yc")
         ys = tile([P, S], U8, "ys")
@@ -166,55 +173,53 @@ def tile_picked_nvp8_none_po_kernel(tc, x_words, x_scales, w1_words, w1_scales, 
         zb = [tile([P, HALF * PACK], BF16, f"zb{h}") for h in range(2)]
         zc = [tile([P, HALF], U32, f"zc{h}") for h in range(2)]
         zs = [tile([P, HALF], U8, f"zs{h}") for h in range(2)]
-        yb = [tile([P, HALF * PACK], BF16, f"yb{h}") for h in range(2)]
-        y = [tile([P, PACK, CH], F32, f"y{c}") for c in range(4)]
+        yb = {1: tile([P, HALF * PACK], BF16, "yb1")}
+        y = [tile([P, PACK, CHUNK], F32, f"y{c}") for c in range(CHUNKS)]
 
         def make_z(c):
-            h, off = divmod(c * CH, HALF)
-            sh = psum.tile([P, PACK, CH], F32, name=f"sh{c}", tag=f"bank{c}")
+            h, off = divmod(c * CHUNK, HALF)
+            sh = psum.tile([P, PACK, CHUNK], F32, name=f"sh{c}", tag=f"bank{c}")
             for t in range(PACK):
                 nc.tensor.matmul_mx(
                     out=sh[:, t, :],
                     lhsT=w2c[:, t * P : (t + 1) * P].bitcast(FP8X4),
                     lhsT_scale=w2s[:, t * P : (t + 1) * P],
-                    rhs=xq[h][:, off : off + CH].bitcast(FP8X4),
-                    rhs_scale=xq_s[:, c * CH : (c + 1) * CH],
+                    rhs=xq[h][:, off : off + CHUNK].bitcast(FP8X4),
+                    rhs_scale=xq_s[:, c * CHUNK : (c + 1) * CHUNK],
                     start=True,
                     stop=True,
                 )
             nc.vector.tensor_tensor(
-                zb[h][:, off * PACK : (off + CH) * PACK].rearrange("p (g i t) -> p g t i", t=PACK, i=2),
+                zb[h][:, off * PACK : (off + CHUNK) * PACK].rearrange("p (g i t) -> p g t i", t=PACK, i=2),
                 sh[:].rearrange("p t (g i) -> p g t i", i=2),
-                prod[h][:, :, off : off + CH].rearrange("p t (g i) -> p g t i", i=2),
+                prod[h][:, :, off : off + CHUNK].rearrange("p t (g i) -> p g t i", i=2),
                 ALU.add,
             )
 
-        def quantise_z(h, off, width):
-            nc.vector.quantize_mx(
-                out=zc[h][:, off : off + width].bitcast(FP8X4), scales=zs[h][:, off : off + width], in_=zb[h][:, off * PACK : (off + width) * PACK]
-            )
-
         def last_layer(c):
-            h, off = divmod(c * CH, HALF)
-            acc = psum.tile([P, PACK, CH], F32, name=f"acc{c}", tag=f"bank{4 + c}")
+            h, off = divmod(c * CHUNK, HALF)
+            codes = zc[h][:, off : off + CHUNK].bitcast(FP8X4)
+            scales = zs[h][:, off : off + CHUNK]
+            nc.vector.quantize_mx(out=codes, scales=scales, in_=zb[h][:, off * PACK : (off + CHUNK) * PACK])
+            acc = psum.tile([P, PACK, CHUNK], F32, name=f"acc{c}", tag=f"bank{CHUNKS + c}")
             for t in range(PACK):
                 nc.tensor.matmul_mx(
                     out=acc[:, t, :],
                     lhsT=w3c[:, t * P : (t + 1) * P].bitcast(FP8X4),
                     lhsT_scale=w3s[:, t * P : (t + 1) * P],
-                    rhs=zc[h][:, off : off + CH].bitcast(FP8X4),
-                    rhs_scale=zs[h][:, off : off + CH],
+                    rhs=codes,
+                    rhs_scale=scales,
                     start=True,
                     stop=True,
                 )
             nc.scalar.copy(out=y[c][:], in_=acc[:])
-            nc.sync.dma_start(out=out_rows[:, :, c * CH : (c + 1) * CH], in_=y[c][:])
+            nc.sync.dma_start(out=out_rows[:, :, c * CHUNK : (c + 1) * CHUNK], in_=y[c][:])
 
         def round_y(c):
-            h, off = divmod(c * CH, HALF)
+            h, off = divmod(c * CHUNK, HALF)
             nc.vector.tensor_copy(
-                out=yb[h][:, off * PACK : (off + CH) * PACK].rearrange("p (g i t) -> p g t i", t=PACK, i=4),
-                in_=y[c][:].rearrange("p t (g i) -> p g t i", i=4),
+                out=yb[h][:, off * PACK : (off + CHUNK) * PACK].rearrange("p (g i t) -> p g t i", t=PACK, i=LINE // 4),
+                in_=y[c][:].rearrange("p t (g i) -> p g t i", i=LINE // 4),
             )
 
         def quantise_y(h, off, width):
@@ -222,25 +227,20 @@ def tile_picked_nvp8_none_po_kernel(tc, x_words, x_scales, w1_words, w1_scales, 
             nc.vector.quantize_mx(out=yc[:, cols].bitcast(FP8X4), scales=ys[:, cols], in_=yb[h][:, off * PACK : (off + width) * PACK])
 
         make_z(0)
-        make_z(1)
-        quantise_z(0, 0, CH)
-        last_layer(0)
-        make_z(2)
-        quantise_z(0, CH, CH)
-        last_layer(1)
-        make_z(3)
-        quantise_z(1, 0, CH)
-        last_layer(2)
-        quantise_z(1, CH, CH)
-        last_layer(3)
-        round_y(0)
-        round_y(1)
-        round_y(2)
+        for c in range(1, CHUNKS):
+            make_z(c)
+            last_layer(c - 1)
+        last_layer(CHUNKS - 1)
+
+        yb[0] = tile([P, HALF * PACK], BF16, "yb0", "zb1")
+        for c in range(CHUNKS - 1):
+            round_y(c)
         quantise_y(0, 0, HALF)
-        round_y(3)
-        quantise_y(1, 0, CH)
-        quantise_y(1, CH, CH)
+        round_y(CHUNKS - 1)
+        quantise_y(1, 0, CHUNK)
+        quantise_y(1, CHUNK, CHUNK)
+
         nc.sync.dma_start(out=out_words, in_=yc[:].bitcast(I32))
-        for q in range(4):
-            queue = nc.scalar if q < 2 else nc.sync
+        for q in range(QUADRANTS):
+            queue = nc.scalar if q < QUADRANTS // 2 else nc.sync
             queue.dma_start(out=out_2[0, 4 * q : 4 * q + 4, :].bitcast(I32), in_=ys[32 * q : 32 * q + 4, :].bitcast(I32))

@@ -236,11 +236,12 @@ def tile_picked_nvp8_none_po_kernel(tc, x_words, x_scales, w1_words, w1_scales, 
         for c in range(CHUNKS - 1):
             round_y(c)
         quantise_y(0, 0, HALF)
+        nc.sync.dma_start(out=out_words[:, :HALF], in_=yc[:, :HALF].bitcast(I32))
         round_y(CHUNKS - 1)
         quantise_y(1, 0, CHUNK)
         quantise_y(1, CHUNK, CHUNK)
 
-        nc.sync.dma_start(out=out_words, in_=yc[:].bitcast(I32))
+        nc.sync.dma_start(out=out_words[:, HALF:], in_=yc[:, HALF:].bitcast(I32))
         for q in range(QUADRANTS):
             queue = nc.scalar if q < QUADRANTS // 2 else nc.sync
             queue.dma_start(out=out_2[0, 4 * q : 4 * q + 4, :].bitcast(I32), in_=ys[32 * q : 32 * q + 4, :].bitcast(I32))

@@ -35,10 +35,10 @@ def load_scales(queue, tile, dram, quadrants):
         queue.dma_start(out=tile[32 * q : 32 * q + 4, :].bitcast(I32), in_=dram[0, 4 * q : 4 * q + 4, :].bitcast(I32))
 
 
-def deal(nc, out, in_, run):
+def deal(nc, out, in_, run, planes=slice(0, PACK)):
     nc.vector.tensor_copy(
-        out=out.rearrange("p (t c m) -> p c t m", t=PACK, m=run),
-        in_=in_.rearrange("p (c m t) -> p c t m", t=PACK, m=run),
+        out=out.rearrange("p (t c m) -> p c t m", t=PACK, m=run)[:, :, planes],
+        in_=in_.rearrange("p (c m t) -> p c t m", t=PACK, m=run)[:, :, planes],
     )
 
 
@@ -60,11 +60,11 @@ def tile_picked_nvp8_none_po_kernel(tc, x_words, x_scales, w1_words, w1_scales, 
         xw = tile([P, T], U32, "xw")
         xs = tile([P, T], U8, "xs")
         w1_raw = staged([P, 4 * H], U32, "w1_raw", 0)[:, :H]
-        w1s_raw = tile([P, H], U8, "w1s_raw")
+        w1s_raw = staged([P, 2 * PLANE_BYTES], U8, "w1s_raw", 4)[:, :H]
         w3s_raw = tile([P, N], U8, "w3s_raw")
 
-        nc.vector.memset(xs[:].bitcast(I32), 0)
-        nc.gpsimd.memset(w1s_raw[:].bitcast(I32), 0)
+        nc.gpsimd.memset(xs[:].bitcast(I32), 0)
+        nc.vector.memset(w1s_raw[:].bitcast(I32), 0)
         nc.gpsimd.memset(w3s_raw[:].bitcast(I32), 0)
 
         other_rows = other.rearrange("(p t) s -> p t s", t=PACK)
@@ -98,11 +98,14 @@ def tile_picked_nvp8_none_po_kernel(tc, x_words, x_scales, w1_words, w1_scales, 
         xq = [tile([P, HALF], U32, "xq0")]
         nc.vector.tensor_copy(out=xq[0][:], in_=xw[:].indirect(offs_t[:, :LIST_HALF]))
         w1s = tile([P, H], U8, "w1s")
-        deal(nc, w1s[:], w1s_raw[:], LINE)
-        xq.append(tile([P, HALF], U32, "xq1", "w1s_raw"))
+        for pair in range(2):
+            deal(nc, w1s[:], w1s_raw[:], LINE, slice(2 * pair, 2 * pair + 2))
+        xq.append(staged([P, HALF], U32, "xq1", 4))
         nc.vector.tensor_copy(out=xq[1][:], in_=xw[:].indirect(offs_t[:, LIST_HALF:]))
         w3c = tile([P, N], U32, "w3c")
         deal(nc, w3c[:], w3_raw[:], LINE // 4)
+        w3s = staged([P, N], U8, "w3s", 5)
+        deal(nc, w3s[:], w3s_raw[:], LINE)
         load_other(2, tile([P, S], F32, "oth2", "xw"))
         load_other(3, staged([P, S], F32, "oth3", 1))
 
@@ -163,8 +166,6 @@ def tile_picked_nvp8_none_po_kernel(tc, x_words, x_scales, w1_words, w1_scales, 
         for step in (tanh_unit, exp_unit, scaled_other):
             for i in range(before_rounding, len(units)):
                 step(i)
-        w3s = tile([P, N], U8, "w3s", f"th{len(units) - 1}")
-        deal(nc, w3s[:], w3s_raw[:], LINE)
 
         yc = tile([P, S], U32, "yc")
         ys = tile([P, S], U8, "ys")

@@ -24,6 +24,8 @@ CHUNKS = S // CHUNK
 LIST_HALF = HALF // 16
 LINE = 16
 PLANE_BYTES = 4 * S
+ALL_PLANES = slice(0, PACK)
+PLANE_PAIRS = (slice(0, 2), slice(2, 4))
 
 
 def words_view(dram):
@@ -35,7 +37,7 @@ def load_scales(queue, tile, dram, quadrants):
         queue.dma_start(out=tile[32 * q : 32 * q + 4, :].bitcast(I32), in_=dram[0, 4 * q : 4 * q + 4, :].bitcast(I32))
 
 
-def deal(nc, out, in_, run, planes=slice(0, PACK)):
+def deal(nc, out, in_, run, planes):
     nc.vector.tensor_copy(
         out=out.rearrange("p (t c m) -> p c t m", t=PACK, m=run)[:, :, planes],
         in_=in_.rearrange("p (c m t) -> p c t m", t=PACK, m=run)[:, :, planes],
@@ -64,7 +66,7 @@ def tile_picked_nvp8_none_po_kernel(tc, x_words, x_scales, w1_words, w1_scales, 
         w3s_raw = tile([P, N], U8, "w3s_raw")
 
         nc.gpsimd.memset(xs[:].bitcast(I32), 0)
-        nc.vector.memset(w1s_raw[:].bitcast(I32), 0)
+        nc.gpsimd.memset(w1s_raw[:].bitcast(I32), 0)
         nc.gpsimd.memset(w3s_raw[:].bitcast(I32), 0)
 
         other_rows = other.rearrange("(p t) s -> p t s", t=PACK)
@@ -85,7 +87,7 @@ def tile_picked_nvp8_none_po_kernel(tc, x_words, x_scales, w1_words, w1_scales, 
             nc.sync.dma_start(out=plane[:], in_=other_rows[:, t, :])
 
         w1c = tile([P, H], U32, "w1c")
-        deal(nc, w1c[:], w1_raw[:], LINE // 4)
+        deal(nc, w1c[:], w1_raw[:], LINE // 4, ALL_PLANES)
         w3_raw = staged([P, N], U32, "w3_raw", 1)
         nc.sync.dma_start(out=w3_raw[:].bitcast(I32), in_=words_view(w3_words))
         load_other(0, staged([P, S], F32, "oth0", 2))
@@ -98,14 +100,14 @@ def tile_picked_nvp8_none_po_kernel(tc, x_words, x_scales, w1_words, w1_scales, 
         xq = [tile([P, HALF], U32, "xq0")]
         nc.vector.tensor_copy(out=xq[0][:], in_=xw[:].indirect(offs_t[:, :LIST_HALF]))
         w1s = tile([P, H], U8, "w1s")
-        for pair in range(2):
-            deal(nc, w1s[:], w1s_raw[:], LINE, slice(2 * pair, 2 * pair + 2))
+        for planes in PLANE_PAIRS:
+            deal(nc, w1s[:], w1s_raw[:], LINE, planes)
         xq.append(staged([P, HALF], U32, "xq1", 4))
         nc.vector.tensor_copy(out=xq[1][:], in_=xw[:].indirect(offs_t[:, LIST_HALF:]))
         w3c = tile([P, N], U32, "w3c")
-        deal(nc, w3c[:], w3_raw[:], LINE // 4)
+        deal(nc, w3c[:], w3_raw[:], LINE // 4, ALL_PLANES)
         w3s = staged([P, N], U8, "w3s", 5)
-        deal(nc, w3s[:], w3s_raw[:], LINE)
+        deal(nc, w3s[:], w3s_raw[:], LINE, ALL_PLANES)
         load_other(2, tile([P, S], F32, "oth2", "xw"))
         load_other(3, staged([P, S], F32, "oth3", 1))
 
@@ -141,8 +143,7 @@ def tile_picked_nvp8_none_po_kernel(tc, x_words, x_scales, w1_words, w1_scales, 
         w2c = tile([P, H], U32, "w2c")
         w2s = tile([P, H], U8, "w2s")
 
-        def round_w2(copy, pair):
-            planes = slice(2 * pair, 2 * pair + 2)
+        def round_w2(copy, planes):
             copy(
                 out=w2b[:].rearrange("p (t m j) -> p m j t", t=PACK, j=PACK)[:, :, :, planes],
                 in_=w2_raw[:].rearrange("p j (m t) -> p m j t", t=PACK)[:, :, :, planes],
@@ -158,8 +159,8 @@ def tile_picked_nvp8_none_po_kernel(tc, x_words, x_scales, w1_words, w1_scales, 
                 scaled_other(i)
         exp_unit(before_rounding - 1)
         w2b = tile([P, H * PACK], BF16, "w2b", f"ex{early_units - 1}")
-        round_w2(nc.vector.tensor_copy, 0)
-        round_w2(nc.scalar.copy, 1)
+        round_w2(nc.vector.tensor_copy, PLANE_PAIRS[0])
+        round_w2(nc.scalar.copy, PLANE_PAIRS[1])
         for i in range(early_units, before_rounding):
             scaled_other(i)
         nc.vector.quantize_mx(out=w2c[:].bitcast(FP8X4), scales=w2s[:], in_=w2b[:])

@@ -3,7 +3,7 @@ from contextlib import ExitStack
 import concourse.mybir as mybir
 
 K, T, S, N, H = 512, 2048, 512, 512, 512
-FLOPS = 3 * 2 * 512 * 512 * 512
+FLOPS = 2 * S * (2 * K * H + H * N)
 
 F32 = mybir.dt.float32
 BF16 = mybir.dt.bfloat16
@@ -54,15 +54,26 @@ def tile_picked_nvp8_none_po_kernel(tc, x_words, x_scales, w1_words, w1_scales, 
         def tile(shape, dt, name, tag=None):
             return keep.tile(shape, dt, name=name, tag=tag or name, align_bytes=64)
 
-        def staged(shape, dt, name, place):
-            return stage.tile(shape, dt, name=name, tag=name, align_bytes=64, offset=PLANE_BYTES * place)
+        def staged(shape, dt, name, place, skip=0):
+            return stage.tile(shape, dt, name=name, tag=name, align_bytes=64, offset=PLANE_BYTES * place + skip)
+
+        def product(out, codes, scales, t, rhs, rhs_scale):
+            nc.tensor.matmul_mx(
+                out=out,
+                lhsT=codes[:, t * P : (t + 1) * P].bitcast(FP8X4),
+                lhsT_scale=scales[:, t * P : (t + 1) * P],
+                rhs=rhs.bitcast(FP8X4),
+                rhs_scale=rhs_scale,
+                start=True,
+                stop=True,
+            )
 
         offs_t = tile([P, S // 16], U16, "offs_t")
         perm_t = tile([P, S // 16], U16, "perm_t")
         xw = tile([P, T], U32, "xw")
         xs = tile([P, T], U8, "xs")
         w1_raw = staged([P, 4 * H], U32, "w1_raw", 0)[:, :H]
-        w1s_raw = staged([P, 2 * PLANE_BYTES], U8, "w1s_raw", 4)[:, :H]
+        w1s_raw = staged([P, H], U8, "w1s_raw", 4)
         w3s_raw = tile([P, N], U8, "w3s_raw")
 
         nc.gpsimd.memset(xs[:].bitcast(I32), 0)
@@ -106,39 +117,31 @@ def tile_picked_nvp8_none_po_kernel(tc, x_words, x_scales, w1_words, w1_scales, 
         nc.vector.tensor_copy(out=xq[1][:], in_=xw[:].indirect(offs_t[:, LIST_HALF:]))
         w3c = tile([P, N], U32, "w3c")
         deal(nc, w3c[:], w3_raw[:], LINE // 4, ALL_PLANES)
-        w3s = staged([P, N], U8, "w3s", 5)
-        deal(nc, w3s[:], w3s_raw[:], LINE, ALL_PLANES)
         load_other(2, tile([P, S], F32, "oth2", "xw"))
         load_other(3, staged([P, S], F32, "oth3", 1))
 
-        prod = [tile([P, PACK, HALF], F32, f"prod{h}") for h in range(2)]
-        units = [(h, 2 * pair + u) for pair in range(2) for h in range(2) for u in range(2)]
+        slots = tile([P, 6 * HALF], F32, "slots")
+        prod = [slots[:, first * HALF : (first + PACK) * HALF].rearrange("p (t s) -> p t s", t=PACK) for first in (2, 0)]
         th = {}
         ex = {}
 
-        def tanh_unit(i):
-            h, t = units[i]
-            bank = psum.tile([P, HALF], F32, name=f"s{i}", tag=f"bank{i}")
-            nc.tensor.matmul_mx(
-                out=bank[:],
-                lhsT=w1c[:, t * P : (t + 1) * P].bitcast(FP8X4),
-                lhsT_scale=w1s[:, t * P : (t + 1) * P],
-                rhs=xq[h][:].bitcast(FP8X4),
-                rhs_scale=xq_s[:, h * HALF : (h + 1) * HALF],
-                start=True,
-                stop=True,
-            )
-            th[i] = tile([P, HALF], F32, f"th{i}")
-            nc.scalar.activation(out=th[i][:], in_=bank[:], func=ACT.Tanh)
+        def looked_up(h, t):
+            return oth[t][:].indirect(perm_t[:, LIST_HALF * h : LIST_HALF * (h + 1)])
 
-        def exp_unit(i):
-            ex[i] = tile([P, HALF], F32, f"ex{i}")
-            nc.scalar.activation(out=ex[i][:], in_=th[i][:], func=ACT.Exp)
+        def tanh_unit(unit, bank_no):
+            h, t = unit
+            bank = psum.tile([P, HALF], F32, name=f"s{h}{t}", tag=f"bank{bank_no}")
+            product(bank[:], w1c, w1s, t, xq[h][:], xq_s[:, h * HALF : (h + 1) * HALF])
+            th[unit] = tile([P, HALF], F32, f"th{h}{t}")
+            nc.scalar.activation(out=th[unit][:], in_=bank[:], func=ACT.Tanh)
 
-        def scaled_other(i):
-            h, t = units[i]
-            lists = perm_t[:, LIST_HALF * h : LIST_HALF * (h + 1)]
-            nc.vector.tensor_tensor(prod[h][:, t, :], oth[t][:].indirect(lists), ex[i][:], ALU.mult)
+        def exp_unit(unit, out):
+            ex[unit] = out
+            nc.scalar.activation(out=out, in_=th[unit][:], func=ACT.Exp)
+
+        def scaled_other(unit):
+            h, t = unit
+            nc.vector.tensor_tensor(prod[h][:, t, :], looked_up(h, t), ex[unit], ALU.mult)
 
         w2c = tile([P, H], U32, "w2c")
         w2s = tile([P, H], U8, "w2s")
@@ -149,48 +152,57 @@ def tile_picked_nvp8_none_po_kernel(tc, x_words, x_scales, w1_words, w1_scales, 
                 in_=w2_raw[:].rearrange("p j (m t) -> p m j t", t=PACK)[:, :, :, planes],
             )
 
-        early_units = len(units) // 2
-        before_rounding = early_units + 2
-        tanh_unit(0)
-        for i in range(before_rounding - 1):
-            tanh_unit(i + 1)
-            exp_unit(i)
-            if i < early_units:
-                scaled_other(i)
-        exp_unit(before_rounding - 1)
-        w2b = tile([P, H * PACK], BF16, "w2b", f"ex{early_units - 1}")
+        units = [(0, 0), (0, 1), (1, 1), (1, 0), (0, 2), (0, 3)]
+        gathered_early, before_quantiser, after_quantiser = units[3:]
+        early = tile([P, HALF], F32, "early")
+        nc.vector.tensor_copy(out=early[:], in_=looked_up(*gathered_early))
+        tanh_unit(units[0], 0)
+        for i, unit in enumerate(units[:4]):
+            tanh_unit(units[i + 1], i + 1)
+            exp_unit(unit, tile([P, HALF], F32, f"ex{i}")[:])
+            if unit != gathered_early:
+                scaled_other(unit)
+        nc.vector.tensor_tensor(prod[1][:, 0, :], early[:], ex[gathered_early], ALU.mult)
+        tanh_unit(after_quantiser, 5)
+        exp_unit(before_quantiser, tile([P, HALF], F32, "ex4")[:])
+
+        w2b = tile([P, H * PACK], BF16, "w2b")
         round_w2(nc.vector.tensor_copy, PLANE_PAIRS[0])
         round_w2(nc.scalar.copy, PLANE_PAIRS[1])
-        for i in range(early_units, before_rounding):
-            scaled_other(i)
+        scaled_other(before_quantiser)
         nc.vector.quantize_mx(out=w2c[:].bitcast(FP8X4), scales=w2s[:], in_=w2b[:])
-        for step in (tanh_unit, exp_unit, scaled_other):
-            for i in range(before_rounding, len(units)):
-                step(i)
+        late = tile([P, 3, HALF], F32, "late", "xs")
+        exp_unit(after_quantiser, late[:, 0, :])
+        scaled_other(after_quantiser)
+        w3s = tile([P, N], U8, "w3s", "w2b")
+        deal(nc, w3s[:], w3s_raw[:], LINE, ALL_PLANES)
 
-        yc = tile([P, S], U32, "yc")
+        last_th = late[:, 1:, :]
+        last_ex = tile([P, 2, HALF], F32, "last_ex")
+        last_other = tile([P, 2, HALF], F32, "last_other", "th03")
+        last_s = psum.tile([P, 2, HALF], F32, name="last_s", tag="bank6")
+        for u in range(2):
+            product(last_s[:, u, :], w1c, w1s, 2 + u, xq[1][:], xq_s[:, HALF:])
+        nc.scalar.activation(out=last_th, in_=last_s[:], func=ACT.Tanh)
+        nc.scalar.activation(out=last_other[:, 0, :], in_=looked_up(1, 2), func=ACT.Copy)
+        nc.scalar.activation(out=last_ex[:], in_=last_th, func=ACT.Exp)
+        nc.scalar.activation(out=last_other[:, 1, :], in_=looked_up(1, 3), func=ACT.Copy)
+
         ys = tile([P, S], U8, "ys")
         out_rows = out_0.rearrange("(p t) s -> p t s", t=PACK)
         out_words = words_view(out_1)
-        zb = [tile([P, HALF * PACK], BF16, f"zb{h}") for h in range(2)]
+        zb = [staged([P, HALF * PACK], BF16, f"zb{h}", 5 + h) for h in range(2)]
         zc = [tile([P, HALF], U32, f"zc{h}") for h in range(2)]
         zs = [tile([P, HALF], U8, f"zs{h}") for h in range(2)]
-        yb = {1: tile([P, HALF * PACK], BF16, "yb1")}
+        yb23 = tile([P, 2 * CHUNK * PACK], BF16, "yb23")
+        yb = {0: tile([P, CHUNK * PACK], BF16, "yb0")[:], 2: yb23[:, : CHUNK * PACK], 3: yb23[:, CHUNK * PACK :]}
         y = [tile([P, PACK, CHUNK], F32, f"y{c}") for c in range(CHUNKS)]
 
         def make_z(c):
             h, off = divmod(c * CHUNK, HALF)
-            sh = psum.tile([P, PACK, CHUNK], F32, name=f"sh{c}", tag=f"bank{c}")
+            sh = psum.tile([P, PACK, CHUNK], F32, name=f"sh{c}", tag=f"bank{c % 2}")
             for t in range(PACK):
-                nc.tensor.matmul_mx(
-                    out=sh[:, t, :],
-                    lhsT=w2c[:, t * P : (t + 1) * P].bitcast(FP8X4),
-                    lhsT_scale=w2s[:, t * P : (t + 1) * P],
-                    rhs=xq[h][:, off : off + CHUNK].bitcast(FP8X4),
-                    rhs_scale=xq_s[:, c * CHUNK : (c + 1) * CHUNK],
-                    start=True,
-                    stop=True,
-                )
+                product(sh[:, t, :], w2c, w2s, t, xq[h][:, off : off + CHUNK], xq_s[:, c * CHUNK : (c + 1) * CHUNK])
             nc.vector.tensor_tensor(
                 zb[h][:, off * PACK : (off + CHUNK) * PACK].rearrange("p (g i t) -> p g t i", t=PACK, i=2),
                 sh[:].rearrange("p t (g i) -> p g t i", i=2),
@@ -198,50 +210,58 @@ def tile_picked_nvp8_none_po_kernel(tc, x_words, x_scales, w1_words, w1_scales, 
                 ALU.add,
             )
 
-        def last_layer(c):
+        def last_layer(c, planes):
             h, off = divmod(c * CHUNK, HALF)
-            codes = zc[h][:, off : off + CHUNK].bitcast(FP8X4)
+            codes = zc[h][:, off : off + CHUNK]
             scales = zs[h][:, off : off + CHUNK]
-            nc.vector.quantize_mx(out=codes, scales=scales, in_=zb[h][:, off * PACK : (off + CHUNK) * PACK])
-            acc = psum.tile([P, PACK, CHUNK], F32, name=f"acc{c}", tag=f"bank{CHUNKS + c}")
+            nc.vector.quantize_mx(out=codes.bitcast(FP8X4), scales=scales, in_=zb[h][:, off * PACK : (off + CHUNK) * PACK])
             for t in range(PACK):
-                nc.tensor.matmul_mx(
-                    out=acc[:, t, :],
-                    lhsT=w3c[:, t * P : (t + 1) * P].bitcast(FP8X4),
-                    lhsT_scale=w3s[:, t * P : (t + 1) * P],
-                    rhs=codes,
-                    rhs_scale=scales,
-                    start=True,
-                    stop=True,
-                )
-            nc.scalar.copy(out=y[c][:], in_=acc[:])
+                product(planes[t], w3c, w3s, t, codes, scales)
+
+        def store_y(c):
             nc.sync.dma_start(out=out_rows[:, :, c * CHUNK : (c + 1) * CHUNK], in_=y[c][:])
 
-        def round_y(c):
-            h, off = divmod(c * CHUNK, HALF)
-            nc.vector.tensor_copy(
-                out=yb[h][:, off * PACK : (off + CHUNK) * PACK].rearrange("p (g i t) -> p g t i", t=PACK, i=LINE // 4),
+        def whole_chunk(c):
+            acc = psum.tile([P, PACK, CHUNK], F32, name=f"acc{c}", tag=f"bank{CHUNKS + c}")
+            last_layer(c, [acc[:, t, :] for t in range(PACK)])
+            nc.scalar.copy(out=y[c][:], in_=acc[:])
+            store_y(c)
+
+        def round_y(copy, c):
+            copy(
+                out=yb[c].rearrange("p (g i t) -> p g t i", t=PACK, i=LINE // 4),
                 in_=y[c][:].rearrange("p t (g i) -> p g t i", i=LINE // 4),
             )
 
-        def quantise_y(h, off, width):
-            cols = slice(h * HALF + off, h * HALF + off + width)
-            nc.vector.quantize_mx(out=yc[:, cols].bitcast(FP8X4), scales=ys[:, cols], in_=yb[h][:, off * PACK : (off + width) * PACK])
+        def quantise_y(c):
+            cols = slice(c * CHUNK, (c + 1) * CHUNK)
+            nc.vector.quantize_mx(out=yc[:, cols].bitcast(FP8X4), scales=ys[:, cols], in_=yb[c])
 
         make_z(0)
-        for c in range(1, CHUNKS):
-            make_z(c)
-            last_layer(c - 1)
-        last_layer(CHUNKS - 1)
+        make_z(1)
+        whole_chunk(0)
+        nc.vector.tensor_tensor(prod[1][:, 2:, :], last_other[:], last_ex[:], ALU.mult)
+        whole_chunk(1)
+        round_y(nc.scalar.copy, 0)
+        make_z(2)
+        make_z(3)
+        whole_chunk(2)
+        pairs = [psum.tile([P, 2, CHUNK], F32, name=f"acc3{u}", tag=f"bank{2 + u}") for u in range(2)]
+        last_layer(3, [pairs[t // 2][:, t % 2, :] for t in range(PACK)])
+        nc.scalar.copy(out=y[3][:, :2, :], in_=pairs[0][:])
 
-        yb[0] = tile([P, HALF * PACK], BF16, "yb0", "zb1")
-        for c in range(CHUNKS - 1):
-            round_y(c)
-        quantise_y(0, 0, HALF)
+        yb[1] = staged([P, CHUNK * PACK], BF16, "yb1", 6)[:]
+        yc = staged([P, S], U32, "yc", 6, PLANE_BYTES // 2)
+        round_y(nc.vector.tensor_copy, 1)
+        quantise_y(0)
+        quantise_y(1)
         nc.sync.dma_start(out=out_words[:, :HALF], in_=yc[:, :HALF].bitcast(I32))
-        round_y(CHUNKS - 1)
-        quantise_y(1, 0, CHUNK)
-        quantise_y(1, CHUNK, CHUNK)
+        nc.vector.tensor_copy(out=y[3][:, 2:, :], in_=pairs[1][:])
+        store_y(3)
+        round_y(nc.vector.tensor_copy, 2)
+        round_y(nc.vector.tensor_copy, 3)
+        quantise_y(2)
+        quantise_y(3)
 
         nc.sync.dma_start(out=out_words[:, HALF:], in_=yc[:, HALF:].bitcast(I32))
         for q in range(QUADRANTS):

@@ -72,13 +72,16 @@ def tile_picked_nvp8_none_po_kernel(tc, x_words, x_scales, w1_words, w1_scales, 
         perm_t = tile([P, S // 16], U16, "perm_t")
         xw = tile([P, T], U32, "xw")
         xs = tile([P, T], U8, "xs")
-        w1_raw = staged([P, 4 * H], U32, "w1_raw", 0)[:, :H]
-        w1s_raw = staged([P, H], U8, "w1s_raw", 4)
+        w1_raw = staged([P, 10 * H], U32, "w1_raw", 0)[:, :H]
+        w1s_raw = staged([P, H], U8, "w1s_raw", 10)
         w3s_raw = tile([P, N], U8, "w3s_raw")
 
         nc.gpsimd.memset(xs[:].bitcast(I32), 0)
         nc.gpsimd.memset(w1s_raw[:].bitcast(I32), 0)
         nc.gpsimd.memset(w3s_raw[:].bitcast(I32), 0)
+        warm_in = tile([P, 8], F32, "warm_in")
+        warm_out = tile([P, 8], F32, "warm_out")
+        nc.gpsimd.memset(warm_in[:], 0.0)
 
         other_rows = other.rearrange("(p t) s -> p t s", t=PACK)
         nc.sync.dma_start(offs_t[:], offs)
@@ -90,122 +93,121 @@ def tile_picked_nvp8_none_po_kernel(tc, x_words, x_scales, w1_words, w1_scales, 
         load_scales(nc.gpsimd, w1s_raw, w1_scales, (3,))
         load_scales(nc.sync, w1s_raw, w1_scales, range(3))
         load_scales(nc.gpsimd, w3s_raw, w3_scales, range(QUADRANTS))
-
-        oth = {}
-
-        def load_other(t, plane):
-            oth[t] = plane
-            nc.sync.dma_start(out=plane[:], in_=other_rows[:, t, :])
+        nc.scalar.activation(out=warm_out[:], in_=warm_in[:], func=ACT.Tanh)
 
         w1c = tile([P, H], U32, "w1c")
         deal(nc, w1c[:], w1_raw[:], LINE // 4, ALL_PLANES)
-        w3_raw = staged([P, N], U32, "w3_raw", 1)
+
+        oth = [staged([P, S], F32, f"oth{t}", 1 + t) for t in range(PACK)]
+        w2_raw = [staged([P, PACK, HALF], F32, f"w2_raw{u}", 5 + 2 * u) for u in range(2)]
+        w3_raw = staged([P, N], U32, "w3_raw", 9)
+        w2_rows = w2.rearrange("(p j) c -> p j c", j=PACK)
+        for t in (0, 1):
+            nc.sync.dma_start(out=oth[t][:], in_=other_rows[:, t, :])
+        for u in range(2):
+            nc.sync.dma_start(out=w2_raw[u][:], in_=w2_rows[:, :, u * HALF : (u + 1) * HALF])
+        for t in (2, 3):
+            nc.sync.dma_start(out=oth[t][:], in_=other_rows[:, t, :])
         nc.sync.dma_start(out=w3_raw[:].bitcast(I32), in_=words_view(w3_words))
-        load_other(0, staged([P, S], F32, "oth0", 2))
-        load_other(1, staged([P, S], F32, "oth1", 3))
 
         xq_s = tile([P, S], U8, "xq_s")
         nc.vector.tensor_copy(out=xq_s[:], in_=xs[:].indirect(offs_t[:]))
-        w2_raw = tile([P, PACK, H], F32, "w2_raw", "xs")
-        nc.sync.dma_start(out=w2_raw[:], in_=w2.rearrange("(p j) c -> p j c", j=PACK))
         xq = [tile([P, HALF], U32, "xq0")]
         nc.vector.tensor_copy(out=xq[0][:], in_=xw[:].indirect(offs_t[:, :LIST_HALF]))
         w1s = tile([P, H], U8, "w1s")
         for planes in PLANE_PAIRS:
             deal(nc, w1s[:], w1s_raw[:], LINE, planes)
-        xq.append(staged([P, HALF], U32, "xq1", 4))
+        xq.append(staged([P, HALF], U32, "xq1", 10))
         nc.vector.tensor_copy(out=xq[1][:], in_=xw[:].indirect(offs_t[:, LIST_HALF:]))
-        w3c = tile([P, N], U32, "w3c")
-        deal(nc, w3c[:], w3_raw[:], LINE // 4, ALL_PLANES)
-        load_other(2, tile([P, S], F32, "oth2", "xw"))
-        load_other(3, staged([P, S], F32, "oth3", 1))
 
-        slots = tile([P, 6 * HALF], F32, "slots")
-        prod = [slots[:, first * HALF : (first + PACK) * HALF].rearrange("p (t s) -> p t s", t=PACK) for first in (2, 0)]
-        th = {}
-        ex = {}
+        pairs = [(h, u) for u in range(2) for h in range(2)]
+        picked = {pr: tile([P, 2, HALF], F32, f"picked{pr[0]}{pr[1]}") for pr in pairs[:3]}
+        th = {(0, u): tile([P, 2, HALF], F32, f"th0{u}") for u in range(2)}
+        ex = {pr: tile([P, 2, HALF], F32, f"ex{pr[0]}{pr[1]}") for pr in pairs}
+        prod = [staged([P, PACK, HALF], F32, f"prod{h}", 7 - 2 * h) for h in range(2)]
 
         def looked_up(h, t):
             return oth[t][:].indirect(perm_t[:, LIST_HALF * h : LIST_HALF * (h + 1)])
 
-        def tanh_unit(unit, bank_no):
-            h, t = unit
-            bank = psum.tile([P, HALF], F32, name=f"s{h}{t}", tag=f"bank{bank_no}")
-            product(bank[:], w1c, w1s, t, xq[h][:], xq_s[:, h * HALF : (h + 1) * HALF])
-            th[unit] = tile([P, HALF], F32, f"th{h}{t}")
-            nc.scalar.activation(out=th[unit][:], in_=bank[:], func=ACT.Tanh)
+        def pick_scalar(h, t):
+            nc.scalar.activation(out=picked[h, t // 2][:, t % 2, :], in_=looked_up(h, t), func=ACT.Copy)
 
-        def exp_unit(unit, out):
-            ex[unit] = out
-            nc.scalar.activation(out=out, in_=th[unit][:], func=ACT.Exp)
+        def pick_vector(h, t):
+            nc.vector.tensor_copy(out=picked[h, t // 2][:, t % 2, :], in_=looked_up(h, t))
 
-        def scaled_other(unit):
-            h, t = unit
-            nc.vector.tensor_tensor(prod[h][:, t, :], looked_up(h, t), ex[unit], ALU.mult)
+        def tanh_pair(h, u):
+            bank = psum.tile([P, 2, HALF], F32, name=f"s{h}{u}", tag=f"bank{2 * h + u}")
+            for i in range(2):
+                product(bank[:, i, :], w1c, w1s, 2 * u + i, xq[h][:], xq_s[:, h * HALF : (h + 1) * HALF])
+            nc.scalar.activation(out=th[h, u][:], in_=bank[:], func=ACT.Tanh)
 
+        def exp_pair(h, u):
+            nc.scalar.activation(out=ex[h, u][:], in_=th[h, u][:], func=ACT.Exp)
+
+        def scale_pair(h, u):
+            nc.vector.tensor_tensor(prod[h][:, 2 * u : 2 * u + 2, :], picked[h, u][:], ex[h, u][:], ALU.mult)
+
+        w2b = staged([P, 2 * H * PACK], BF16, "w2b", 13)[:, : H * PACK]
         w2c = tile([P, H], U32, "w2c")
         w2s = tile([P, H], U8, "w2s")
 
-        def round_w2(copy, planes):
+        def round_w2(copy, u):
             copy(
-                out=w2b[:].rearrange("p (t m j) -> p m j t", t=PACK, j=PACK)[:, :, :, planes],
-                in_=w2_raw[:].rearrange("p j (m t) -> p m j t", t=PACK)[:, :, :, planes],
+                out=w2b[:].rearrange("p (t m j) -> p m j t", t=PACK, j=PACK)[:, u * P // 2 : (u + 1) * P // 2],
+                in_=w2_raw[u][:].rearrange("p j (m t) -> p m j t", t=PACK),
             )
 
-        units = [(0, 0), (0, 1), (1, 1), (1, 0), (0, 2), (0, 3)]
-        gathered_early, before_quantiser, after_quantiser = units[3:]
-        early = tile([P, HALF], F32, "early")
-        nc.vector.tensor_copy(out=early[:], in_=looked_up(*gathered_early))
-        tanh_unit(units[0], 0)
-        for i, unit in enumerate(units[:4]):
-            tanh_unit(units[i + 1], i + 1)
-            exp_unit(unit, tile([P, HALF], F32, f"ex{i}")[:])
-            if unit != gathered_early:
-                scaled_other(unit)
-        nc.vector.tensor_tensor(prod[1][:, 0, :], early[:], ex[gathered_early], ALU.mult)
-        tanh_unit(after_quantiser, 5)
-        exp_unit(before_quantiser, tile([P, HALF], F32, "ex4")[:])
-
-        w2b = tile([P, H * PACK], BF16, "w2b")
-        round_w2(nc.vector.tensor_copy, PLANE_PAIRS[0])
-        round_w2(nc.scalar.copy, PLANE_PAIRS[1])
-        scaled_other(before_quantiser)
+        pick_scalar(0, 0)
+        pick_scalar(1, 0)
+        pick_vector(0, 1)
+        pick_vector(1, 1)
+        tanh_pair(0, 0)
+        tanh_pair(0, 1)
+        exp_pair(0, 0)
+        exp_pair(0, 1)
+        pick_scalar(0, 2)
+        pick_scalar(0, 3)
+        round_w2(nc.vector.tensor_copy, 0)
+        round_w2(nc.vector.tensor_copy, 1)
+        scale_pair(0, 0)
         nc.vector.quantize_mx(out=w2c[:].bitcast(FP8X4), scales=w2s[:], in_=w2b[:])
-        late = tile([P, 3, HALF], F32, "late", "xs")
-        exp_unit(after_quantiser, late[:, 0, :])
-        scaled_other(after_quantiser)
-        w3s = tile([P, N], U8, "w3s", "w2b")
+        w3c = tile([P, N], U32, "w3c")
+        deal(nc, w3c[:], w3_raw[:], LINE // 4, ALL_PLANES)
+        scale_pair(0, 1)
+        w3s = staged([P, N], U8, "w3s", 16)
         deal(nc, w3s[:], w3s_raw[:], LINE, ALL_PLANES)
-
-        last_th = late[:, 1:, :]
-        last_ex = tile([P, 2, HALF], F32, "last_ex")
-        last_other = tile([P, 2, HALF], F32, "last_other", "th03")
-        last_s = psum.tile([P, 2, HALF], F32, name="last_s", tag="bank6")
-        for u in range(2):
-            product(last_s[:, u, :], w1c, w1s, 2 + u, xq[1][:], xq_s[:, HALF:])
-        nc.scalar.activation(out=last_th, in_=last_s[:], func=ACT.Tanh)
-        nc.scalar.activation(out=last_other[:, 0, :], in_=looked_up(1, 2), func=ACT.Copy)
-        nc.scalar.activation(out=last_ex[:], in_=last_th, func=ACT.Exp)
-        nc.scalar.activation(out=last_other[:, 1, :], in_=looked_up(1, 3), func=ACT.Copy)
+        th[1, 0] = staged([P, 2, HALF], F32, "th10", 13)
+        th[1, 1] = staged([P, 2, HALF], F32, "th11", 14)
+        picked[1, 1] = staged([P, 2, HALF], F32, "picked11", 15)
+        tanh_pair(1, 0)
+        tanh_pair(1, 1)
+        exp_pair(1, 0)
+        pick_scalar(1, 2)
+        exp_pair(1, 1)
 
         ys = tile([P, S], U8, "ys")
         out_rows = out_0.rearrange("(p t) s -> p t s", t=PACK)
         out_words = words_view(out_1)
-        zb = [staged([P, HALF * PACK], BF16, f"zb{h}", 5 + h) for h in range(2)]
+        zb = [staged([P, HALF * PACK], BF16, f"zb{h}", place) for h, place in enumerate((9, 12))]
         zc = [tile([P, HALF], U32, f"zc{h}") for h in range(2)]
         zs = [tile([P, HALF], U8, f"zs{h}") for h in range(2)]
         yb23 = tile([P, 2 * CHUNK * PACK], BF16, "yb23")
         yb = {0: tile([P, CHUNK * PACK], BF16, "yb0")[:], 2: yb23[:, : CHUNK * PACK], 3: yb23[:, CHUNK * PACK :]}
         y = [tile([P, PACK, CHUNK], F32, f"y{c}") for c in range(CHUNKS)]
 
+        sh = {}
+
+        def shift(c, bank_no):
+            h, off = divmod(c * CHUNK, HALF)
+            sh[c] = psum.tile([P, PACK, CHUNK], F32, name=f"sh{c}", tag=f"bank{bank_no}")
+            for t in range(PACK):
+                product(sh[c][:, t, :], w2c, w2s, t, xq[h][:, off : off + CHUNK], xq_s[:, c * CHUNK : (c + 1) * CHUNK])
+
         def make_z(c):
             h, off = divmod(c * CHUNK, HALF)
-            sh = psum.tile([P, PACK, CHUNK], F32, name=f"sh{c}", tag=f"bank{c % 2}")
-            for t in range(PACK):
-                product(sh[:, t, :], w2c, w2s, t, xq[h][:, off : off + CHUNK], xq_s[:, c * CHUNK : (c + 1) * CHUNK])
             nc.vector.tensor_tensor(
                 zb[h][:, off * PACK : (off + CHUNK) * PACK].rearrange("p (g i t) -> p g t i", t=PACK, i=2),
-                sh[:].rearrange("p t (g i) -> p g t i", i=2),
+                sh[c][:].rearrange("p t (g i) -> p g t i", i=2),
                 prod[h][:, :, off : off + CHUNK].rearrange("p t (g i) -> p g t i", i=2),
                 ALU.add,
             )
@@ -221,8 +223,8 @@ def tile_picked_nvp8_none_po_kernel(tc, x_words, x_scales, w1_words, w1_scales, 
         def store_y(c):
             nc.sync.dma_start(out=out_rows[:, :, c * CHUNK : (c + 1) * CHUNK], in_=y[c][:])
 
-        def whole_chunk(c):
-            acc = psum.tile([P, PACK, CHUNK], F32, name=f"acc{c}", tag=f"bank{CHUNKS + c}")
+        def whole_chunk(c, bank_no):
+            acc = psum.tile([P, PACK, CHUNK], F32, name=f"acc{c}", tag=f"bank{bank_no}")
             last_layer(c, [acc[:, t, :] for t in range(PACK)])
             nc.scalar.copy(out=y[c][:], in_=acc[:])
             store_y(c)
@@ -237,26 +239,30 @@ def tile_picked_nvp8_none_po_kernel(tc, x_words, x_scales, w1_words, w1_scales, 
             cols = slice(c * CHUNK, (c + 1) * CHUNK)
             nc.vector.quantize_mx(out=yc[:, cols].bitcast(FP8X4), scales=ys[:, cols], in_=yb[c])
 
+        for c, bank_no in enumerate((4, 5, 0, 1)):
+            shift(c, bank_no)
         make_z(0)
         make_z(1)
-        whole_chunk(0)
-        nc.vector.tensor_tensor(prod[1][:, 2:, :], last_other[:], last_ex[:], ALU.mult)
-        whole_chunk(1)
+        pick_vector(1, 3)
+        whole_chunk(0, 6)
+        scale_pair(1, 0)
+        whole_chunk(1, 7)
+        scale_pair(1, 1)
         round_y(nc.scalar.copy, 0)
         make_z(2)
         make_z(3)
-        whole_chunk(2)
-        pairs = [psum.tile([P, 2, CHUNK], F32, name=f"acc3{u}", tag=f"bank{2 + u}") for u in range(2)]
-        last_layer(3, [pairs[t // 2][:, t % 2, :] for t in range(PACK)])
-        nc.scalar.copy(out=y[3][:, :2, :], in_=pairs[0][:])
+        whole_chunk(2, 2)
+        halves = [psum.tile([P, 2, CHUNK], F32, name=f"acc3{u}", tag=f"bank{4 + u}") for u in range(2)]
+        last_layer(3, [halves[t // 2][:, t % 2, :] for t in range(PACK)])
+        nc.scalar.copy(out=y[3][:, :2, :], in_=halves[0][:])
 
-        yb[1] = staged([P, CHUNK * PACK], BF16, "yb1", 6)[:]
-        yc = staged([P, S], U32, "yc", 6, PLANE_BYTES // 2)
+        yb[1] = staged([P, CHUNK * PACK], BF16, "yb1", 12)[:]
+        yc = staged([P, S], U32, "yc", 12, PLANE_BYTES // 2)
         round_y(nc.vector.tensor_copy, 1)
         quantise_y(0)
         quantise_y(1)
         nc.sync.dma_start(out=out_words[:, :HALF], in_=yc[:, :HALF].bitcast(I32))
-        nc.vector.tensor_copy(out=y[3][:, 2:, :], in_=pairs[1][:])
+        nc.vector.tensor_copy(out=y[3][:, 2:, :], in_=halves[1][:])
         store_y(3)
         round_y(nc.vector.tensor_copy, 2)
         round_y(nc.vector.tensor_copy, 3)

@@ -106,9 +106,9 @@ def tile_picked_nvp8_none_po_kernel(tc, x_words, x_scales, w1_words, w1_scales, 
             nc.sync.dma_start(out=oth[t][:], in_=other_rows[:, t, :])
         for u in range(2):
             nc.sync.dma_start(out=w2_raw[u][:], in_=w2_rows[:, :, u * HALF : (u + 1) * HALF])
+        nc.sync.dma_start(out=w3_raw[:].bitcast(I32), in_=words_view(w3_words))
         for t in (2, 3):
             nc.sync.dma_start(out=oth[t][:], in_=other_rows[:, t, :])
-        nc.sync.dma_start(out=w3_raw[:].bitcast(I32), in_=words_view(w3_words))
 
         xq_s = tile([P, S], U8, "xq_s")
         nc.vector.tensor_copy(out=xq_s[:], in_=xs[:].indirect(offs_t[:]))
@@ -169,21 +169,21 @@ def tile_picked_nvp8_none_po_kernel(tc, x_words, x_scales, w1_words, w1_scales, 
         pick_scalar(0, 3)
         round_w2(nc.vector.tensor_copy, 0)
         round_w2(nc.vector.tensor_copy, 1)
-        scale_pair(0, 0)
-        nc.vector.quantize_mx(out=w2c[:].bitcast(FP8X4), scales=w2s[:], in_=w2b[:])
         w3c = tile([P, N], U32, "w3c")
         deal(nc, w3c[:], w3_raw[:], LINE // 4, ALL_PLANES)
+        nc.vector.quantize_mx(out=w2c[:].bitcast(FP8X4), scales=w2s[:], in_=w2b[:])
+        scale_pair(0, 0)
         scale_pair(0, 1)
         w3s = staged([P, N], U8, "w3s", 16)
         deal(nc, w3s[:], w3s_raw[:], LINE, ALL_PLANES)
-        th[1, 0] = staged([P, 2, HALF], F32, "th10", 13)
-        th[1, 1] = staged([P, 2, HALF], F32, "th11", 14)
-        picked[1, 1] = staged([P, 2, HALF], F32, "picked11", 15)
+        th[1, 0] = tile([P, 2, HALF], F32, "th10", "picked00")
+        th[1, 1] = tile([P, 2, HALF], F32, "th11", "ex00")
+        picked12 = tile([P, HALF], F32, "picked12", "picked01")
         tanh_pair(1, 0)
         tanh_pair(1, 1)
         exp_pair(1, 0)
-        pick_scalar(1, 2)
         exp_pair(1, 1)
+        nc.scalar.activation(out=picked12[:], in_=looked_up(1, 2), func=ACT.Copy)
 
         ys = tile([P, S], U8, "ys")
         out_rows = out_0.rearrange("(p t) s -> p t s", t=PACK)
@@ -192,7 +192,7 @@ def tile_picked_nvp8_none_po_kernel(tc, x_words, x_scales, w1_words, w1_scales, 
         zc = [tile([P, HALF], U32, f"zc{h}") for h in range(2)]
         zs = [tile([P, HALF], U8, f"zs{h}") for h in range(2)]
         yb23 = tile([P, 2 * CHUNK * PACK], BF16, "yb23")
-        yb = {0: tile([P, CHUNK * PACK], BF16, "yb0")[:], 2: yb23[:, : CHUNK * PACK], 3: yb23[:, CHUNK * PACK :]}
+        yb = {0: tile([P, CHUNK * PACK], BF16, "yb0")[:], 1: tile([P, CHUNK * PACK], BF16, "yb1")[:], 2: yb23[:, : CHUNK * PACK], 3: yb23[:, CHUNK * PACK :]}
         y = [tile([P, PACK, CHUNK], F32, f"y{c}") for c in range(CHUNKS)]
 
         sh = {}
@@ -239,26 +239,34 @@ def tile_picked_nvp8_none_po_kernel(tc, x_words, x_scales, w1_words, w1_scales, 
             cols = slice(c * CHUNK, (c + 1) * CHUNK)
             nc.vector.quantize_mx(out=yc[:, cols].bitcast(FP8X4), scales=ys[:, cols], in_=yb[c])
 
-        for c, bank_no in enumerate((4, 5, 0, 1)):
-            shift(c, bank_no)
+        shift(0, 4)
+        shift(1, 5)
         make_z(0)
         make_z(1)
-        pick_vector(1, 3)
         whole_chunk(0, 6)
+        shift(2, 5)
         scale_pair(1, 0)
         whole_chunk(1, 7)
-        scale_pair(1, 1)
+        shift(3, 6)
+
+        def last_plane(c):
+            off = c * CHUNK - HALF
+            window = oth[3][:].indirect(perm_t[:, c * CHUNK // 16 : (c + 1) * CHUNK // 16])
+            nc.vector.tensor_tensor(prod[1][:, 3, off : off + CHUNK], window, ex[1, 1][:, 1, off : off + CHUNK], ALU.mult)
+
+        last_plane(2)
+        nc.vector.tensor_tensor(prod[1][:, 2, :], picked12[:], ex[1, 1][:, 0, :], ALU.mult)
+        last_plane(3)
         round_y(nc.scalar.copy, 0)
+        round_y(nc.scalar.copy, 1)
         make_z(2)
         make_z(3)
         whole_chunk(2, 2)
-        halves = [psum.tile([P, 2, CHUNK], F32, name=f"acc3{u}", tag=f"bank{4 + u}") for u in range(2)]
+        halves = [psum.tile([P, 2, CHUNK], F32, name=f"acc3{u}", tag=f"bank{u}") for u in range(2)]
         last_layer(3, [halves[t // 2][:, t % 2, :] for t in range(PACK)])
         nc.scalar.copy(out=y[3][:, :2, :], in_=halves[0][:])
 
-        yb[1] = staged([P, CHUNK * PACK], BF16, "yb1", 12)[:]
-        yc = staged([P, S], U32, "yc", 12, PLANE_BYTES // 2)
-        round_y(nc.vector.tensor_copy, 1)
+        yc = staged([P, S], U32, "yc", 12)
         quantise_y(0)
         quantise_y(1)
         nc.sync.dma_start(out=out_words[:, :HALF], in_=yc[:, :HALF].bitcast(I32))

@@ -37,8 +37,8 @@ def load_scales(queue, tile, dram, quadrants):
         queue.dma_start(out=tile[32 * q : 32 * q + 4, :].bitcast(I32), in_=dram[0, 4 * q : 4 * q + 4, :].bitcast(I32))
 
 
-def deal(nc, out, in_, run, planes):
-    nc.vector.tensor_copy(
+def deal(copy, out, in_, run, planes):
+    copy(
         out=out.rearrange("p (t c m) -> p c t m", t=PACK, m=run)[:, :, planes],
         in_=in_.rearrange("p (c m t) -> p c t m", t=PACK, m=run)[:, :, planes],
     )
@@ -72,31 +72,34 @@ def tile_picked_nvp8_none_po_kernel(tc, x_words, x_scales, w1_words, w1_scales, 
         perm_t = tile([P, S // 16], U16, "perm_t")
         xw = tile([P, T], U32, "xw")
         xs = tile([P, T], U8, "xs")
-        w1_raw = staged([P, 10 * H], U32, "w1_raw", 0)[:, :H]
+        xs_rows = tile([P, T], U8, "xs_rows")
+        w1_raw = staged([P, H], U32, "w1_raw", 0)
         w1s_raw = staged([P, H], U8, "w1s_raw", 10)
         w3s_raw = tile([P, N], U8, "w3s_raw")
 
-        nc.gpsimd.memset(xs[:].bitcast(I32), 0)
         nc.gpsimd.memset(w1s_raw[:].bitcast(I32), 0)
+        nc.gpsimd.memset(xs[:].bitcast(I32), 0)
         nc.gpsimd.memset(w3s_raw[:].bitcast(I32), 0)
         warm_in = tile([P, 8], F32, "warm_in")
         warm_out = tile([P, 8], F32, "warm_out")
         nc.gpsimd.memset(warm_in[:], 0.0)
 
         other_rows = other.rearrange("(p t) s -> p t s", t=PACK)
+        load_scales(nc.scalar, xs_rows, x_scales, (0, 1))
+        load_scales(nc.sync, xs_rows, x_scales, (2, 3))
+        load_scales(nc.scalar, w1s_raw, w1_scales, (0,))
         nc.sync.dma_start(offs_t[:], offs)
         nc.sync.dma_start(perm_t[:], perm)
-        nc.sync.dma_start(out=w1_raw[:].bitcast(I32), in_=words_view(w1_words))
-        load_scales(nc.scalar, xs, x_scales, (0, 1))
-        load_scales(nc.sync, xs, x_scales, (2, 3))
         nc.sync.dma_start(out=xw[:].bitcast(I32), in_=words_view(x_words))
-        load_scales(nc.gpsimd, w1s_raw, w1_scales, (3,))
-        load_scales(nc.sync, w1s_raw, w1_scales, range(3))
+        nc.sync.dma_start(out=w1_raw[:].bitcast(I32), in_=words_view(w1_words))
+        load_scales(nc.sync, w1s_raw, w1_scales, (1, 2, 3))
         load_scales(nc.gpsimd, w3s_raw, w3_scales, range(QUADRANTS))
         nc.scalar.activation(out=warm_out[:], in_=warm_in[:], func=ACT.Tanh)
 
         w1c = tile([P, H], U32, "w1c")
-        deal(nc, w1c[:], w1_raw[:], LINE // 4, ALL_PLANES)
+        for q in range(QUADRANTS):
+            rows = slice(32 * q, 32 * q + 4)
+            nc.vector.tensor_copy(out=xs[rows, :].bitcast(I32), in_=xs_rows[rows, :].bitcast(I32))
 
         oth = [staged([P, S], F32, f"oth{t}", 1 + t) for t in range(PACK)]
         w2_raw = [staged([P, PACK, HALF], F32, f"w2_raw{u}", 5 + 2 * u) for u in range(2)]
@@ -116,7 +119,8 @@ def tile_picked_nvp8_none_po_kernel(tc, x_words, x_scales, w1_words, w1_scales, 
         nc.vector.tensor_copy(out=xq[0][:], in_=xw[:].indirect(offs_t[:, :LIST_HALF]))
         w1s = tile([P, H], U8, "w1s")
         for planes in PLANE_PAIRS:
-            deal(nc, w1s[:], w1s_raw[:], LINE, planes)
+            deal(nc.vector.tensor_copy, w1s[:], w1s_raw[:], LINE, planes)
+        deal(nc.scalar.copy, w1c[:], w1_raw[:], LINE // 4, ALL_PLANES)
         xq.append(staged([P, HALF], U32, "xq1", 10))
         nc.vector.tensor_copy(out=xq[1][:], in_=xw[:].indirect(offs_t[:, LIST_HALF:]))
 
@@ -170,12 +174,12 @@ def tile_picked_nvp8_none_po_kernel(tc, x_words, x_scales, w1_words, w1_scales, 
         round_w2(nc.vector.tensor_copy, 0)
         round_w2(nc.vector.tensor_copy, 1)
         w3c = tile([P, N], U32, "w3c")
-        deal(nc, w3c[:], w3_raw[:], LINE // 4, ALL_PLANES)
+        deal(nc.vector.tensor_copy, w3c[:], w3_raw[:], LINE // 4, ALL_PLANES)
         nc.vector.quantize_mx(out=w2c[:].bitcast(FP8X4), scales=w2s[:], in_=w2b[:])
         scale_pair(0, 0)
         scale_pair(0, 1)
         w3s = staged([P, N], U8, "w3s", 16)
-        deal(nc, w3s[:], w3s_raw[:], LINE, ALL_PLANES)
+        deal(nc.vector.tensor_copy, w3s[:], w3s_raw[:], LINE, ALL_PLANES)
         th[1, 0] = tile([P, 2, HALF], F32, "th10", "picked00")
         th[1, 1] = tile([P, 2, HALF], F32, "th11", "ex00")
         picked12 = tile([P, HALF], F32, "picked12", "picked01")

@@ -93,7 +93,6 @@ def tile_picked_nvp8_none_po_kernel(tc, x_words, x_scales, w1_words, w1_scales, 
         nc.sync.dma_start(out=xw[:].bitcast(I32), in_=words_view(x_words))
         nc.sync.dma_start(out=w1_raw[:].bitcast(I32), in_=words_view(w1_words))
         load_scales(nc.sync, w1s_raw, w1_scales, (1, 2, 3))
-        load_scales(nc.gpsimd, w3s_raw, w3_scales, range(QUADRANTS))
         nc.scalar.activation(out=warm_out[:], in_=warm_in[:], func=ACT.Tanh)
 
         w1c = tile([P, H], U32, "w1c")
@@ -112,6 +111,7 @@ def tile_picked_nvp8_none_po_kernel(tc, x_words, x_scales, w1_words, w1_scales, 
         nc.sync.dma_start(out=w3_raw[:].bitcast(I32), in_=words_view(w3_words))
         for t in (2, 3):
             nc.sync.dma_start(out=oth[t][:], in_=other_rows[:, t, :])
+        load_scales(nc.sync, w3s_raw, w3_scales, range(QUADRANTS))
 
         xq_s = tile([P, S], U8, "xq_s")
         nc.vector.tensor_copy(out=xq_s[:], in_=xs[:].indirect(offs_t[:]))
@@ -177,9 +177,11 @@ def tile_picked_nvp8_none_po_kernel(tc, x_words, x_scales, w1_words, w1_scales, 
         deal(nc.vector.tensor_copy, w3c[:], w3_raw[:], LINE // 4, ALL_PLANES)
         nc.vector.quantize_mx(out=w2c[:].bitcast(FP8X4), scales=w2s[:], in_=w2b[:])
         scale_pair(0, 0)
-        scale_pair(0, 1)
-        w3s = staged([P, N], U8, "w3s", 16)
-        deal(nc.vector.tensor_copy, w3s[:], w3s_raw[:], LINE, ALL_PLANES)
+        for off in (0, CHUNK):
+            cols = slice(off, off + CHUNK)
+            nc.vector.tensor_tensor(prod[0][:, 2:, cols], picked[0, 1][:, :, cols], ex[0, 1][:, :, cols], ALU.mult)
+        w3s = tile([P, N], U8, "w3s", "ex01")
+        deal(nc.gpsimd.tensor_copy, w3s[:], w3s_raw[:], LINE, ALL_PLANES)
         th[1, 0] = tile([P, 2, HALF], F32, "th10", "picked00")
         th[1, 1] = tile([P, 2, HALF], F32, "th11", "ex00")
         picked12 = tile([P, HALF], F32, "picked12", "picked01")

@@ -85,8 +85,8 @@ def tile_picked_nvp8_none_po_kernel(tc, x_words, x_scales, w1_words, w1_scales, 
         nc.gpsimd.memset(warm_in[:], 0.0)
 
         other_rows = other.rearrange("(p t) s -> p t s", t=PACK)
-        load_scales(nc.scalar, xs_rows, x_scales, (0, 1))
-        load_scales(nc.sync, xs_rows, x_scales, (2, 3))
+        load_scales(nc.sync, xs_rows, x_scales, (0, 2))
+        load_scales(nc.scalar, xs_rows, x_scales, (1, 3))
         load_scales(nc.scalar, w1s_raw, w1_scales, (0,))
         nc.sync.dma_start(offs_t[:], offs)
         nc.sync.dma_start(perm_t[:], perm)
@@ -96,7 +96,7 @@ def tile_picked_nvp8_none_po_kernel(tc, x_words, x_scales, w1_words, w1_scales, 
         nc.scalar.activation(out=warm_out[:], in_=warm_in[:], func=ACT.Tanh)
 
         w1c = tile([P, H], U32, "w1c")
-        for q in range(QUADRANTS):
+        for q in (0, 2, 1, 3):
             rows = slice(32 * q, 32 * q + 4)
             nc.vector.tensor_copy(out=xs[rows, :].bitcast(I32), in_=xs_rows[rows, :].bitcast(I32))
 
@@ -181,7 +181,7 @@ def tile_picked_nvp8_none_po_kernel(tc, x_words, x_scales, w1_words, w1_scales, 
             cols = slice(off, off + CHUNK)
             nc.vector.tensor_tensor(prod[0][:, 2:, cols], picked[0, 1][:, :, cols], ex[0, 1][:, :, cols], ALU.mult)
         w3s = tile([P, N], U8, "w3s", "ex01")
-        deal(nc.gpsimd.tensor_copy, w3s[:], w3s_raw[:], LINE, ALL_PLANES)
+        nc.gpsimd.tensor_copy(out=w3s[:].rearrange("p (t m) -> p t m", t=PACK), in_=w3s_raw[:].rearrange("p (m t) -> p t m", t=PACK))
         th[1, 0] = tile([P, 2, HALF], F32, "th10", "picked00")
         th[1, 1] = tile([P, 2, HALF], F32, "th11", "ex00")
         picked12 = tile([P, HALF], F32, "picked12", "picked01")

@@ -77,12 +77,12 @@ def tile_picked_nvp8_none_po_kernel(tc, x_words, x_scales, w1_words, w1_scales, 
         w1s_raw = staged([P, H], U8, "w1s_raw", 10)
         w3s_raw = tile([P, N], U8, "w3s_raw")
 
-        nc.gpsimd.memset(w1s_raw[:].bitcast(I32), 0)
-        nc.gpsimd.memset(xs[:].bitcast(I32), 0)
-        nc.gpsimd.memset(w3s_raw[:].bitcast(I32), 0)
         warm_in = tile([P, 8], F32, "warm_in")
         warm_out = tile([P, 8], F32, "warm_out")
-        nc.gpsimd.memset(warm_in[:], 0.0)
+        nc.vector.memset(w1s_raw[:].bitcast(I32), 0)
+        nc.vector.memset(warm_in[:], 0.0)
+        nc.vector.memset(xs[:].bitcast(I32), 0)
+        nc.vector.memset(w3s_raw[:].bitcast(I32), 0)
 
         other_rows = other.rearrange("(p t) s -> p t s", t=PACK)
         load_scales(nc.sync, xs_rows, x_scales, (0, 2))

@@ -24,8 +24,9 @@ CHUNKS = S // CHUNK
 LIST_HALF = HALF // 16
 LINE = 16
 PLANE_BYTES = 4 * S
+W2_FIRST = 320
+W2_PIECES = (slice(0, W2_FIRST), slice(W2_FIRST, H))
 ALL_PLANES = slice(0, PACK)
-PLANE_PAIRS = (slice(0, 2), slice(2, 4))
 
 
 def words_view(dram):
@@ -101,13 +102,13 @@ def tile_picked_nvp8_none_po_kernel(tc, x_words, x_scales, w1_words, w1_scales, 
             nc.vector.tensor_copy(out=xs[rows, :].bitcast(I32), in_=xs_rows[rows, :].bitcast(I32))
 
         oth = [staged([P, S], F32, f"oth{t}", 1 + t) for t in range(PACK)]
-        w2_raw = [staged([P, PACK, HALF], F32, f"w2_raw{u}", 5 + 2 * u) for u in range(2)]
+        w2_raw = [staged([P, PACK, W2_FIRST], F32, "w2_raw0", 5), staged([P, PACK, H - W2_FIRST], F32, "w2_raw1", 7, 16 * (W2_FIRST - HALF))]
         w3_raw = staged([P, N], U32, "w3_raw", 9)
         w2_rows = w2.rearrange("(p j) c -> p j c", j=PACK)
         for t in (0, 1):
             nc.sync.dma_start(out=oth[t][:], in_=other_rows[:, t, :])
         for u in range(2):
-            nc.sync.dma_start(out=w2_raw[u][:], in_=w2_rows[:, :, u * HALF : (u + 1) * HALF])
+            nc.sync.dma_start(out=w2_raw[u][:], in_=w2_rows[:, :, W2_PIECES[u]])
         nc.sync.dma_start(out=w3_raw[:].bitcast(I32), in_=words_view(w3_words))
         for t in (2, 3):
             nc.sync.dma_start(out=oth[t][:], in_=other_rows[:, t, :])
@@ -118,8 +119,7 @@ def tile_picked_nvp8_none_po_kernel(tc, x_words, x_scales, w1_words, w1_scales, 
         xq = [tile([P, HALF], U32, "xq0")]
         nc.vector.tensor_copy(out=xq[0][:], in_=xw[:].indirect(offs_t[:, :LIST_HALF]))
         w1s = tile([P, H], U8, "w1s")
-        for planes in PLANE_PAIRS:
-            deal(nc.vector.tensor_copy, w1s[:], w1s_raw[:], LINE, planes)
+        deal(nc.vector.tensor_copy, w1s[:], w1s_raw[:], LINE, ALL_PLANES)
         deal(nc.scalar.copy, w1c[:], w1_raw[:], LINE // 4, ALL_PLANES)
         xq.append(staged([P, HALF], U32, "xq1", 10))
         nc.vector.tensor_copy(out=xq[1][:], in_=xw[:].indirect(offs_t[:, LIST_HALF:]))
@@ -132,6 +132,9 @@ def tile_picked_nvp8_none_po_kernel(tc, x_words, x_scales, w1_words, w1_scales, 
 
         def looked_up(h, t):
             return oth[t][:].indirect(perm_t[:, LIST_HALF * h : LIST_HALF * (h + 1)])
+
+        def chunk_of(c, t):
+            return oth[t][:].indirect(perm_t[:, c * CHUNK // 16 : (c + 1) * CHUNK // 16])
 
         def pick_scalar(h, t):
             nc.scalar.activation(out=picked[h, t // 2][:, t % 2, :], in_=looked_up(h, t), func=ACT.Copy)
@@ -157,7 +160,7 @@ def tile_picked_nvp8_none_po_kernel(tc, x_words, x_scales, w1_words, w1_scales, 
 
         def round_w2(copy, u):
             copy(
-                out=w2b[:].rearrange("p (t m j) -> p m j t", t=PACK, j=PACK)[:, u * P // 2 : (u + 1) * P // 2],
+                out=w2b[:].rearrange("p (t m j) -> p m j t", t=PACK, j=PACK)[:, W2_PIECES[u].start // PACK : W2_PIECES[u].stop // PACK],
                 in_=w2_raw[u][:].rearrange("p j (m t) -> p m j t", t=PACK),
             )
 
@@ -170,26 +173,28 @@ def tile_picked_nvp8_none_po_kernel(tc, x_words, x_scales, w1_words, w1_scales, 
         exp_pair(0, 0)
         exp_pair(0, 1)
         pick_scalar(0, 2)
-        pick_scalar(0, 3)
         round_w2(nc.vector.tensor_copy, 0)
         round_w2(nc.vector.tensor_copy, 1)
         w3c = tile([P, N], U32, "w3c")
         deal(nc.vector.tensor_copy, w3c[:], w3_raw[:], LINE // 4, ALL_PLANES)
-        nc.vector.quantize_mx(out=w2c[:].bitcast(FP8X4), scales=w2s[:], in_=w2b[:])
         scale_pair(0, 0)
-        for off in (0, CHUNK):
-            cols = slice(off, off + CHUNK)
-            nc.vector.tensor_tensor(prod[0][:, 2:, cols], picked[0, 1][:, :, cols], ex[0, 1][:, :, cols], ALU.mult)
+        nc.vector.quantize_mx(out=w2c[:].bitcast(FP8X4), scales=w2s[:], in_=w2b[:])
+        nc.vector.tensor_tensor(prod[0][:, 2, :], picked[0, 1][:, 0, :], ex[0, 1][:, 0, :], ALU.mult)
+        for c in range(2):
+            cols = slice(c * CHUNK, (c + 1) * CHUNK)
+            nc.vector.tensor_tensor(prod[0][:, 3, cols], chunk_of(c, 3), ex[0, 1][:, 1, cols], ALU.mult)
         w3s = tile([P, N], U8, "w3s", "ex01")
         nc.gpsimd.tensor_copy(out=w3s[:].rearrange("p (t m) -> p t m", t=PACK), in_=w3s_raw[:].rearrange("p (m t) -> p t m", t=PACK))
         th[1, 0] = tile([P, 2, HALF], F32, "th10", "picked00")
         th[1, 1] = tile([P, 2, HALF], F32, "th11", "ex00")
-        picked12 = tile([P, HALF], F32, "picked12", "picked01")
+        picked[1, 1] = tile([P, 2, HALF], F32, "picked11", "picked01")
         tanh_pair(1, 0)
         tanh_pair(1, 1)
         exp_pair(1, 0)
         exp_pair(1, 1)
-        nc.scalar.activation(out=picked12[:], in_=looked_up(1, 2), func=ACT.Copy)
+        for c in (2, 3):
+            for t in (2, 3):
+                nc.scalar.activation(out=picked[1, 1][:, t - 2, (c - 2) * CHUNK : (c - 1) * CHUNK], in_=chunk_of(c, t), func=ACT.Copy)
 
         ys = tile([P, S], U8, "ys")
         out_rows = out_0.rearrange("(p t) s -> p t s", t=PACK)
@@ -253,31 +258,26 @@ def tile_picked_nvp8_none_po_kernel(tc, x_words, x_scales, w1_words, w1_scales, 
         shift(2, 5)
         scale_pair(1, 0)
         whole_chunk(1, 7)
-        shift(3, 6)
-
-        def last_plane(c):
-            off = c * CHUNK - HALF
-            window = oth[3][:].indirect(perm_t[:, c * CHUNK // 16 : (c + 1) * CHUNK // 16])
-            nc.vector.tensor_tensor(prod[1][:, 3, off : off + CHUNK], window, ex[1, 1][:, 1, off : off + CHUNK], ALU.mult)
-
-        last_plane(2)
-        nc.vector.tensor_tensor(prod[1][:, 2, :], picked12[:], ex[1, 1][:, 0, :], ALU.mult)
-        last_plane(3)
+        shift(3, 4)
+        for off in (0, CHUNK):
+            cols = slice(off, off + CHUNK)
+            nc.vector.tensor_tensor(prod[1][:, 2:, cols], picked[1, 1][:, :, cols], ex[1, 1][:, :, cols], ALU.mult)
+            make_z(2 + off // CHUNK)
         round_y(nc.scalar.copy, 0)
         round_y(nc.scalar.copy, 1)
-        make_z(2)
-        make_z(3)
-        whole_chunk(2, 2)
-        halves = [psum.tile([P, 2, CHUNK], F32, name=f"acc3{u}", tag=f"bank{u}") for u in range(2)]
-        last_layer(3, [halves[t // 2][:, t % 2, :] for t in range(PACK)])
-        nc.scalar.copy(out=y[3][:, :2, :], in_=halves[0][:])
+        halves = {}
+        for c, first_bank in ((2, 2), (3, 0)):
+            halves[c] = [psum.tile([P, 2, CHUNK], F32, name=f"acc{c}{u}", tag=f"bank{first_bank + u}") for u in range(2)]
+            last_layer(c, [halves[c][t // 2][:, t % 2, :] for t in range(PACK)])
+            nc.scalar.copy(out=y[c][:, 2:, :], in_=halves[c][1][:])
 
         yc = staged([P, S], U32, "yc", 12)
         quantise_y(0)
         quantise_y(1)
         nc.sync.dma_start(out=out_words[:, :HALF], in_=yc[:, :HALF].bitcast(I32))
-        nc.vector.tensor_copy(out=y[3][:, 2:, :], in_=halves[1][:])
-        store_y(3)
+        for c in (2, 3):
+            nc.vector.tensor_copy(out=y[c][:, :2, :], in_=halves[c][0][:])
+            store_y(c)
         round_y(nc.vector.tensor_copy, 2)
         round_y(nc.vector.tensor_copy, 3)
         quantise_y(2)

from contextlib import ExitStack

import concourse.mybir as mybir

K, T, S, N, H = 512, 2048, 512, 512, 512
FLOPS = 2 * S * (2 * K * H + H * N)

F32 = mybir.dt.float32
BF16 = mybir.dt.bfloat16
I32 = mybir.dt.int32
U32 = mybir.dt.uint32
U16 = mybir.dt.uint16
U8 = mybir.dt.uint8
FP8X4 = mybir.dt.float8_e4m3fn_x4
ACT = mybir.ActivationFunctionType
ALU = mybir.AluOpType

P = 128
PACK = 4
QUADRANTS = 4
HALF = 256
CHUNK = 128
CHUNKS = S // CHUNK
LIST_HALF = HALF // 16
LINE = 16
PLANE_BYTES = 4 * S
W2_FIRST = 320
W2_PIECES = (slice(0, W2_FIRST), slice(W2_FIRST, H))
ALL_PLANES = slice(0, PACK)


def words_view(dram):
    return dram[0].rearrange("p n t -> p (n t)").bitcast(I32)


def load_scales(queue, tile, dram, quadrants):
    for q in quadrants:
        queue.dma_start(out=tile[32 * q : 32 * q + 4, :].bitcast(I32), in_=dram[0, 4 * q : 4 * q + 4, :].bitcast(I32))


def deal(copy, out, in_, run, planes):
    copy(
        out=out.rearrange("p (t c m) -> p c t m", t=PACK, m=run)[:, :, planes],
        in_=in_.rearrange("p (c m t) -> p c t m", t=PACK, m=run)[:, :, planes],
    )


def tile_picked_nvp8_none_po_kernel(tc, x_words, x_scales, w1_words, w1_scales, w2, other, w3_words, w3_scales, offs, perm, out_0, out_1, out_2):
    nc = tc.nc
    with ExitStack() as ctx:
        keep = ctx.enter_context(tc.tile_pool(name="keep", bufs=1))
        stage = ctx.enter_context(tc.tile_pool(name="stage", bufs=1))
        psum = ctx.enter_context(tc.psum_pool(name="psum", bufs=1))

        def tile(shape, dt, name, tag=None):
            return keep.tile(shape, dt, name=name, tag=tag or name, align_bytes=64)

        def staged(shape, dt, name, place, skip=0):
            return stage.tile(shape, dt, name=name, tag=name, align_bytes=64, offset=PLANE_BYTES * place + skip)

        def product(out, codes, scales, t, rhs, rhs_scale):
            nc.tensor.matmul_mx(
                out=out,
                lhsT=codes[:, t * P : (t + 1) * P].bitcast(FP8X4),
                lhsT_scale=scales[:, t * P : (t + 1) * P],
                rhs=rhs.bitcast(FP8X4),
                rhs_scale=rhs_scale,
                start=True,
                stop=True,
            )

        offs_t = tile([P, S // 16], U16, "offs_t")
        perm_t = tile([P, S // 16], U16, "perm_t")
        xw = tile([P, T], U32, "xw")
        xs = tile([P, T], U8, "xs")
        xs_rows = tile([P, T], U8, "xs_rows")
        w1_raw = staged([P, H], U32, "w1_raw", 0)
        w1s_raw = staged([P, H], U8, "w1s_raw", 10)
        w3s_raw = tile([P, N], U8, "w3s_raw")

        warm_in = tile([P, 8], F32, "warm_in")
        warm_out = tile([P, 8], F32, "warm_out")
        nc.vector.memset(w1s_raw[:].bitcast(I32), 0)
        nc.vector.memset(warm_in[:], 0.0)
        nc.vector.memset(xs[:].bitcast(I32), 0)
        nc.vector.memset(w3s_raw[:].bitcast(I32), 0)

        other_rows = other.rearrange("(p t) s -> p t s", t=PACK)
        load_scales(nc.sync, xs_rows, x_scales, (0, 2))
        load_scales(nc.scalar, xs_rows, x_scales, (1, 3))
        load_scales(nc.scalar, w1s_raw, w1_scales, (0,))
        nc.sync.dma_start(offs_t[:], offs)
        nc.sync.dma_start(perm_t[:], perm)
        nc.sync.dma_start(out=xw[:].bitcast(I32), in_=words_view(x_words))
        nc.sync.dma_start(out=w1_raw[:].bitcast(I32), in_=words_view(w1_words))
        load_scales(nc.sync, w1s_raw, w1_scales, (1, 2, 3))
        nc.scalar.activation(out=warm_out[:], in_=warm_in[:], func=ACT.Tanh)

        w1c = tile([P, H], U32, "w1c")
        for q in (0, 2, 1, 3):
            rows = slice(32 * q, 32 * q + 4)
            nc.vector.tensor_copy(out=xs[rows, :].bitcast(I32), in_=xs_rows[rows, :].bitcast(I32))

        oth = [staged([P, S], F32, f"oth{t}", 1 + t) for t in range(PACK)]
        w2_raw = [staged([P, PACK, W2_FIRST], F32, "w2_raw0", 5), staged([P, PACK, H - W2_FIRST], F32, "w2_raw1", 7, 16 * (W2_FIRST - HALF))]
        w3_raw = staged([P, N], U32, "w3_raw", 9)
        w2_rows = w2.rearrange("(p j) c -> p j c", j=PACK)
        for t in (0, 1):
            nc.sync.dma_start(out=oth[t][:], in_=other_rows[:, t, :])
        for u in range(2):
            nc.sync.dma_start(out=w2_raw[u][:], in_=w2_rows[:, :, W2_PIECES[u]])
        nc.sync.dma_start(out=w3_raw[:].bitcast(I32), in_=words_view(w3_words))
        for t in (2, 3):
            nc.sync.dma_start(out=oth[t][:], in_=other_rows[:, t, :])
        load_scales(nc.sync, w3s_raw, w3_scales, range(QUADRANTS))

        xq_s = tile([P, S], U8, "xq_s")
        nc.vector.tensor_copy(out=xq_s[:], in_=xs[:].indirect(offs_t[:]))
        xq = [tile([P, HALF], U32, "xq0")]
        nc.vector.tensor_copy(out=xq[0][:], in_=xw[:].indirect(offs_t[:, :LIST_HALF]))
        w1s = tile([P, H], U8, "w1s")
        deal(nc.vector.tensor_copy, w1s[:], w1s_raw[:], LINE, ALL_PLANES)
        deal(nc.scalar.copy, w1c[:], w1_raw[:], LINE // 4, ALL_PLANES)
        xq.append(staged([P, HALF], U32, "xq1", 10))
        nc.vector.tensor_copy(out=xq[1][:], in_=xw[:].indirect(offs_t[:, LIST_HALF:]))

        pairs = [(h, u) for u in range(2) for h in range(2)]
        picked = {pr: tile([P, 2, HALF], F32, f"picked{pr[0]}{pr[1]}") for pr in pairs[:3]}
        th = {(0, u): tile([P, 2, HALF], F32, f"th0{u}") for u in range(2)}
        ex = {pr: tile([P, 2, HALF], F32, f"ex{pr[0]}{pr[1]}") for pr in pairs}
        prod = [staged([P, PACK, HALF], F32, f"prod{h}", 7 - 2 * h) for h in range(2)]

        def looked_up(h, t):
            return oth[t][:].indirect(perm_t[:, LIST_HALF * h : LIST_HALF * (h + 1)])

        def chunk_of(c, t):
            return oth[t][:].indirect(perm_t[:, c * CHUNK // 16 : (c + 1) * CHUNK // 16])

        def pick_scalar(h, t):
            nc.scalar.activation(out=picked[h, t // 2][:, t % 2, :], in_=looked_up(h, t), func=ACT.Copy)

        def pick_vector(h, t):
            nc.vector.tensor_copy(out=picked[h, t // 2][:, t % 2, :], in_=looked_up(h, t))

        def tanh_pair(h, u):
            bank = psum.tile([P, 2, HALF], F32, name=f"s{h}{u}", tag=f"bank{2 * h + u}")
            for i in range(2):
                product(bank[:, i, :], w1c, w1s, 2 * u + i, xq[h][:], xq_s[:, h * HALF : (h + 1) * HALF])
            nc.scalar.activation(out=th[h, u][:], in_=bank[:], func=ACT.Tanh)

        def exp_pair(h, u):
            nc.scalar.activation(out=ex[h, u][:], in_=th[h, u][:], func=ACT.Exp)

        def scale_pair(h, u):
            nc.vector.tensor_tensor(prod[h][:, 2 * u : 2 * u + 2, :], picked[h, u][:], ex[h, u][:], ALU.mult)

        w2b = staged([P, 2 * H * PACK], BF16, "w2b", 13)[:, : H * PACK]
        w2c = tile([P, H], U32, "w2c")
        w2s = tile([P, H], U8, "w2s")

        def round_w2(copy, u):
            copy(
                out=w2b[:].rearrange("p (t m j) -> p m j t", t=PACK, j=PACK)[:, W2_PIECES[u].start // PACK : W2_PIECES[u].stop // PACK],
                in_=w2_raw[u][:].rearrange("p j (m t) -> p m j t", t=PACK),
            )

        pick_scalar(0, 0)
        pick_scalar(1, 0)
        pick_vector(0, 1)
        pick_vector(1, 1)
        tanh_pair(0, 0)
        tanh_pair(0, 1)
        exp_pair(0, 0)
        exp_pair(0, 1)
        pick_scalar(0, 2)
        round_w2(nc.vector.tensor_copy, 0)
        round_w2(nc.vector.tensor_copy, 1)
        w3c = tile([P, N], U32, "w3c")
        deal(nc.vector.tensor_copy, w3c[:], w3_raw[:], LINE // 4, ALL_PLANES)
        scale_pair(0, 0)
        nc.vector.quantize_mx(out=w2c[:].bitcast(FP8X4), scales=w2s[:], in_=w2b[:])
        nc.vector.tensor_tensor(prod[0][:, 2, :], picked[0, 1][:, 0, :], ex[0, 1][:, 0, :], ALU.mult)
        for c in range(2):
            cols = slice(c * CHUNK, (c + 1) * CHUNK)
            nc.vector.tensor_tensor(prod[0][:, 3, cols], chunk_of(c, 3), ex[0, 1][:, 1, cols], ALU.mult)
        w3s = tile([P, N], U8, "w3s", "ex01")
        nc.gpsimd.tensor_copy(out=w3s[:].rearrange("p (t m) -> p t m", t=PACK), in_=w3s_raw[:].rearrange("p (m t) -> p t m", t=PACK))
        th[1, 0] = tile([P, 2, HALF], F32, "th10", "picked00")
        th[1, 1] = tile([P, 2, HALF], F32, "th11", "ex00")
        picked[1, 1] = tile([P, 2, HALF], F32, "picked11", "picked01")
        tanh_pair(1, 0)
        tanh_pair(1, 1)
        exp_pair(1, 0)
        exp_pair(1, 1)
        for c in (2, 3):
            for t in (2, 3):
                nc.scalar.activation(out=picked[1, 1][:, t - 2, (c - 2) * CHUNK : (c - 1) * CHUNK], in_=chunk_of(c, t), func=ACT.Copy)

        ys = tile([P, S], U8, "ys")
        out_rows = out_0.rearrange("(p t) s -> p t s", t=PACK)
        out_words = words_view(out_1)
        zb = [staged([P, HALF * PACK], BF16, f"zb{h}", place) for h, place in enumerate((9, 12))]
        zc = [tile([P, HALF], U32, f"zc{h}") for h in range(2)]
        zs = [tile([P, HALF], U8, f"zs{h}") for h in range(2)]
        yb23 = tile([P, 2 * CHUNK * PACK], BF16, "yb23")
        yb = {0: tile([P, CHUNK * PACK], BF16, "yb0")[:], 1: tile([P, CHUNK * PACK], BF16, "yb1")[:], 2: yb23[:, : CHUNK * PACK], 3: yb23[:, CHUNK * PACK :]}
        y = [tile([P, PACK, CHUNK], F32, f"y{c}") for c in range(CHUNKS)]

        sh = {}

        def shift(c, bank_no):
            h, off = divmod(c * CHUNK, HALF)
            sh[c] = psum.tile([P, PACK, CHUNK], F32, name=f"sh{c}", tag=f"bank{bank_no}")
            for t in range(PACK):
                product(sh[c][:, t, :], w2c, w2s, t, xq[h][:, off : off + CHUNK], xq_s[:, c * CHUNK : (c + 1) * CHUNK])

        def make_z(c):
            h, off = divmod(c * CHUNK, HALF)
            nc.vector.tensor_tensor(
                zb[h][:, off * PACK : (off + CHUNK) * PACK].rearrange("p (g i t) -> p g t i", t=PACK, i=2),
                sh[c][:].rearrange("p t (g i) -> p g t i", i=2),
                prod[h][:, :, off : off + CHUNK].rearrange("p t (g i) -> p g t i", i=2),
                ALU.add,
            )

        def last_layer(c, planes):
            h, off = divmod(c * CHUNK, HALF)
            codes = zc[h][:, off : off + CHUNK]
            scales = zs[h][:, off : off + CHUNK]
            nc.vector.quantize_mx(out=codes.bitcast(FP8X4), scales=scales, in_=zb[h][:, off * PACK : (off + CHUNK) * PACK])
            for t in range(PACK):
                product(planes[t], w3c, w3s, t, codes, scales)

        def store_y(c):
            nc.sync.dma_start(out=out_rows[:, :, c * CHUNK : (c + 1) * CHUNK], in_=y[c][:])

        def whole_chunk(c, bank_no):
            acc = psum.tile([P, PACK, CHUNK], F32, name=f"acc{c}", tag=f"bank{bank_no}")
            last_layer(c, [acc[:, t, :] for t in range(PACK)])
            nc.scalar.copy(out=y[c][:], in_=acc[:])
            store_y(c)

        def round_y(copy, c):
            copy(
                out=yb[c].rearrange("p (g i t) -> p g t i", t=PACK, i=LINE // 4),
                in_=y[c][:].rearrange("p t (g i) -> p g t i", i=LINE // 4),
            )

        def quantise_y(c):
            cols = slice(c * CHUNK, (c + 1) * CHUNK)
            nc.vector.quantize_mx(out=yc[:, cols].bitcast(FP8X4), scales=ys[:, cols], in_=yb[c])

        shift(0, 4)
        shift(1, 5)
        make_z(0)
        make_z(1)
        whole_chunk(0, 6)
        shift(2, 5)
        scale_pair(1, 0)
        whole_chunk(1, 7)
        shift(3, 4)
        for off in (0, CHUNK):
            cols = slice(off, off + CHUNK)
            nc.vector.tensor_tensor(prod[1][:, 2:, cols], picked[1, 1][:, :, cols], ex[1, 1][:, :, cols], ALU.mult)
            make_z(2 + off // CHUNK)
        round_y(nc.scalar.copy, 0)
        round_y(nc.scalar.copy, 1)
        halves = {}
        for c, first_bank in ((2, 2), (3, 0)):
            halves[c] = [psum.tile([P, 2, CHUNK], F32, name=f"acc{c}{u}", tag=f"bank{first_bank + u}") for u in range(2)]
            last_layer(c, [halves[c][t // 2][:, t % 2, :] for t in range(PACK)])
            nc.scalar.copy(out=y[c][:, 2:, :], in_=halves[c][1][:])

        yc = staged([P, S], U32, "yc", 12)
        quantise_y(0)
        quantise_y(1)
        nc.sync.dma_start(out=out_words[:, :HALF], in_=yc[:, :HALF].bitcast(I32))
        for c in (2, 3):
            nc.vector.tensor_copy(out=y[c][:, :2, :], in_=halves[c][0][:])
            store_y(c)
        round_y(nc.vector.tensor_copy, 2)
        round_y(nc.vector.tensor_copy, 3)
        quantise_y(2)
        quantise_y(3)

        nc.sync.dma_start(out=out_words[:, HALF:], in_=yc[:, HALF:].bitcast(I32))
        for q in range(QUADRANTS):
            queue = nc.scalar if q < QUADRANTS // 2 else nc.sync
            queue.dma_start(out=out_2[0, 4 * q : 4 * q + 4, :].bitcast(I32), in_=ys[32 * q : 32 * q + 4, :].bitcast(I32))
